import numpy as np
import ml_dtypes


def mxq(x, axis, fmt="e4m3"):
    dtype, down = {"e4m3": (ml_dtypes.float8_e4m3fn, 7), "e5m2": (ml_dtypes.float8_e5m2, 14)}[fmt]
    v = np.moveaxis(np.asarray(x, np.float32).astype(ml_dtypes.bfloat16).astype(np.float64), axis, -1)
    blocks = v.reshape(v.shape[:-1] + (-1, 32))
    amax = np.abs(blocks).max(-1, keepdims=True)
    byte = np.maximum(np.where(amax > 0, np.frexp(amax)[1] - 1 + 127, 0) - down, 1)
    scale = np.exp2(byte - 127.0)
    codes = (blocks / scale).astype(np.float32).astype(dtype).astype(np.float64)
    return np.moveaxis((codes * scale).reshape(v.shape), -1, axis)


WIDE = False


def mx_kscale(k):
    if not WIDE:
        return np.ones(k)
    levels = np.array([10, -10, 5, -5, 0])
    if k % 512:
        return np.exp2(np.random.permutation(np.resize(levels, k // 32))).repeat(32)
    a = np.empty((k // 512, 16))
    for p in range(k // 512):
        a[p, :8] = np.random.permutation(np.resize(levels, 8))
        for g in range(8):
            far = levels[np.abs(levels - a[p, g]) >= 10]
            a[p, g + 8] = far[np.random.randint(len(far))]
    return np.exp2(a.ravel()).repeat(32)


def f64(x):
    return np.asarray(x).astype(np.float64)


def striped(idx):
    return np.tile(np.asarray(idx).reshape(-1, 16).T, (8, 1)).astype(np.uint16)


def unstriped(offs):
    return offs[:16].T.reshape(-1).astype(np.int64)


E2M1 = np.array([0.0, 0.5, 1.0, 1.5, 2.0, 3.0, 4.0, 6.0, -0.0, -0.5, -1.0, -1.5, -2.0, -3.0, -4.0, -6.0])


def pack_weight(w, fmt):
    k, n = w.shape
    w = f64(np.asarray(w, np.float32).astype(ml_dtypes.bfloat16)).reshape(k // 32, 32, n)
    amax = np.abs(w).max(1)
    if fmt == "e4m3":
        byte = np.frexp(amax)[1] - 1 + 127 - 7
    else:
        mant, ex = np.frexp(amax / 6.0)
        byte = np.where(mant > 0.5, ex, ex - 1) + 127
    byte = np.clip(np.where(amax > 0, byte, 1), 1, 254)
    scaled = (w * np.exp2(127.0 - byte)[:, None, :]).reshape(k, n).astype(np.float32)
    by_word = np.ascontiguousarray(scaled.reshape(k // 512, 128, 4, n).transpose(0, 1, 3, 2))
    if fmt == "e4m3":
        words = by_word.astype(ml_dtypes.float8_e4m3fn).view(np.uint8)
    else:
        c = by_word.astype(ml_dtypes.float4_e2m1fn).view(np.uint8) & 0xF
        words = (c[..., 0::2] | (c[..., 1::2] << 4)).reshape(k // 512, 128, 2 * n)
    return np.ascontiguousarray(words), np.ascontiguousarray(byte.astype(np.uint8).reshape(k // 512, 16, n))


def unpack_weight(words, scales, fmt):
    g, _, n = scales.shape
    words = np.ascontiguousarray(words).reshape(g, 128, n, -1)
    if fmt == "e4m3":
        vals = words.view(ml_dtypes.float8_e4m3fn).astype(np.float64)
    else:
        nib = np.empty((g, 128, n, 4), np.uint8)
        nib[..., 0::2] = words & 0xF
        nib[..., 1::2] = words >> 4
        vals = E2M1[nib]
    vals = vals * np.repeat(np.exp2(scales.astype(np.float64) - 127.0), 8, axis=1)[..., None]
    return vals.transpose(0, 1, 3, 2).reshape(g * 512, n)


D, T, I, U, J, Q = 512, 2048, 512, 2048, 512, 128


def setup_inputs():
    n = np.random.standard_normal
    idx = np.random.permutation(T)[:I]
    idx2 = np.random.permutation(U)[:J]
    fd = mx_kscale(D)
    fi = mx_kscale(I)
    keysp = pack_weight(n((D, T)) / fd[:, None], "e4m3")
    qpoolp = pack_weight(n((D, T)) * 0.6 / np.sqrt(D) * fd[:, None], "e4m3")
    keys2p = pack_weight(n((D, U)) / fd[:, None], "e4m3")
    return {
        "query": (n((D, Q)) * 0.6 / np.sqrt(D) * fd[:, None]).astype(np.float32),
        "keys_words": keysp[0],
        "keys_scales": keysp[1],
        "qpool_words": qpoolp[0],
        "qpool_scales": qpoolp[1],
        "keys2_words": keys2p[0],
        "keys2_scales": keys2p[1],
        "sa": (np.random.uniform(0.5, 2.0, (1, I)) * fi).astype(np.float32),
        "sb": (np.random.uniform(0.5, 2.0, (I, 1)) / fi[:, None]).astype(np.float32),
        "offs": striped(idx),
        "offs2": striped(idx2),
    }


def reference(query, keys_words, keys_scales, qpool_words, qpool_scales, keys2_words, keys2_scales, sa, sb, offs, offs2):
    idx = unstriped(offs)
    idx2 = unstriped(offs2)
    keysu = unpack_weight(keys_words, keys_scales, "e4m3")
    qpoolu = unpack_weight(qpool_words, qpool_scales, "e4m3")
    keys2u = unpack_weight(keys2_words, keys2_scales, "e4m3")
    queryq = mxq(f64(query), 0, "e4m3")
    keysidxg = keysu[:, idx]
    a = queryq.T @ keysidxg
    p = np.exp(a - np.max(a, axis=1, keepdims=True))
    w = p * f64(sa) / np.sum(p, axis=1, keepdims=True)
    wt = w.T
    qpoolidxg = qpoolu[:, idx]
    keys2idx2g = keys2u[:, idx2]
    b = qpoolidxg.T @ keys2idx2g
    r = np.exp(b - np.max(b, axis=1, keepdims=True))
    x = r * f64(sb) / np.sum(r, axis=1, keepdims=True) * 512.0
    wtq = mxq(wt, 0, "e4m3")
    xq = mxq(x, 0, "e4m3")
    y = wtq.T @ xq
    return y

@@ -1,0 +1,217 @@
+from contextlib import ExitStack
+
+import concourse.mybir as mybir
+
+F32 = mybir.dt.float32
+BF16 = mybir.dt.bfloat16
+I32 = mybir.dt.int32
+U32 = mybir.dt.uint32
+U16 = mybir.dt.uint16
+U8 = mybir.dt.uint8
+FP8X4 = mybir.dt.float8_e4m3fn_x4
+ALU = mybir.AluOpType
+ACT = mybir.ActivationFunctionType
+AXIS_X = mybir.AxisListType.X
+
+P = 128
+PACK = 4
+D, T, I, J, Q = 512, 2048, 512, 512, 128
+HALF = J // 2
+RUN = 4
+FLOPS = 2 * D * Q * I + 2 * D * I * J + 2 * I * Q * J
+
+KEYS_ROW, QPOOL_ROW, KEYS2_ROW = 0, 8, 4
+
+
+def load_words(nc, tile, words):
+    nc.sync.dma_start(out=tile[:].bitcast(I32), in_=words[0].rearrange("p n t -> p (n t)").bitcast(I32))
+
+
+def load_scales(nc, tile, scales, row):
+    rows = scales[0].bitcast(I32)
+    for quad in range(4):
+        first = 32 * quad + row
+        nc.sync.dma_start(out=tile[first : first + 4, :].bitcast(I32), in_=rows[4 * quad : 4 * quad + 4, :])
+
+
+def tile_attend_rollout_kernel(
+    tc, query, keys_words, keys_scales, qpool_words, qpool_scales, keys2_words, keys2_scales, sa, sb, offs, offs2, out
+):
+    nc = tc.nc
+    with ExitStack() as ctx:
+        keep = ctx.enter_context(tc.tile_pool(name="keep", bufs=1))
+        big = ctx.enter_context(tc.tile_pool(name="big", bufs=1))
+        psum = ctx.enter_context(tc.psum_pool(name="psum", bufs=1))
+
+        offs_t = keep.tile([P, I // 16], U16, name="offs_t")
+        offs2_t = keep.tile([P, J // 16], U16, name="offs2_t")
+        k_sc = keep.tile([P, T], U8, name="k_sc", align_bytes=64)
+        qp_sc = keep.tile([P, T], U8, name="qp_sc", align_bytes=64)
+        k2_sc = keep.tile([P, T], U8, name="k2_sc", align_bytes=64)
+        ident = keep.tile([P, P], F32, name="ident")
+        slot_rows = keep.tile([P, P], F32, name="slot_rows")
+
+        win = 4 * T
+        zeros = big.tile([P, P], F32, name="zeros", offset=win - 256)
+        q_raw = big.tile([P, PACK, Q], F32, name="q_raw", offset=2 * win)
+
+        for plane in (k_sc, qp_sc, k2_sc):
+            nc.vector.memset(plane[:].bitcast(I32), 0)
+        nc.gpsimd.memset(zeros[:], 0.0)
+        nc.gpsimd.affine_select(
+            out=ident[:], in_=zeros[:], compare_op=ALU.not_equal, fill=1.0, base=0, pattern=[[-1, P]], channel_multiplier=1
+        )
+        nc.gpsimd.memset(slot_rows[:], 0.0)
+
+        k_w = big.tile([P, T], U32, name="k_w", offset=0)
+        qp_w = big.tile([P, T], U32, name="qp_w", offset=win)
+
+        nc.sync.dma_start(offs_t[:], offs)
+        nc.sync.dma_start(out=q_raw[:], in_=query.rearrange("(p j) w -> p j w", j=PACK))
+        nc.sync.dma_start(offs2_t[:], offs2)
+        load_scales(nc, k_sc, keys_scales, KEYS_ROW)
+        load_words(nc, k_w, keys_words)
+        load_scales(nc, qp_sc, qpool_scales, QPOOL_ROW)
+        nc.sync.dma_start(
+            out=slot_rows[0:PACK, :].rearrange("t (m r) -> t m r", r=RUN),
+            in_=sb.rearrange("(m t r) o -> t m (r o)", t=PACK, r=RUN),
+        )
+        nc.sync.dma_start(
+            out=slot_rows[PACK : 2 * PACK, :].rearrange("t (m r) -> t m r", r=RUN),
+            in_=sa.rearrange("o (m t r) -> t (o m) r", t=PACK, r=RUN),
+        )
+        load_words(nc, qp_w, qpool_words)
+        load_scales(nc, k2_sc, keys2_scales, KEYS2_ROW)
+
+        q_grp = keep.tile([P, Q, PACK], BF16, name="q_grp", align_bytes=64)
+        nc.scalar.copy(out=q_grp[:], in_=q_raw[:].rearrange("p j w -> p w j"))
+
+        k2_w = big.tile([P, T], U32, name="k2_w", offset=2 * win)
+        load_words(nc, k2_w, keys2_words)
+
+        cols_ps = psum.tile([P, P], F32, name="cols_ps", tag="bank_c")
+        nc.tensor.transpose(cols_ps[:], slot_rows[:], ident[:])
+        sb_col = keep.tile([P, PACK], F32, name="sb_col")
+        sa_col = keep.tile([P, PACK], F32, name="sa_col")
+        nc.scalar.activation(out=sb_col[:], in_=cols_ps[:, 0:PACK], func=ACT.Copy, scale=512.0)
+        nc.scalar.copy(out=sa_col[:], in_=cols_ps[:, PACK : 2 * PACK])
+
+        kg_sc = keep.tile([P, I], U8, name="kg_sc", align_bytes=64)
+        nc.vector.tensor_copy(kg_sc[:], k_sc[:].indirect(offs_t[:]))
+        q_codes = keep.tile([P, Q], U32, name="q_codes", align_bytes=64)
+        q_sc = keep.tile([P, Q], U8, name="q_sc", align_bytes=64)
+        nc.vector.quantize_mx(out=q_codes[:].bitcast(FP8X4), scales=q_sc[:], in_=q_grp[:].rearrange("p w j -> p (w j)"))
+        kg_w = keep.tile([P, I], U32, name="kg_w", align_bytes=64)
+        nc.vector.tensor_copy(kg_w[:], k_w[:].indirect(offs_t[:]))
+        a_ps = psum.tile([P, I], F32, name="a_ps", tag="bank_a")
+        nc.tensor.matmul_mx(
+            out=a_ps[:], lhsT=q_codes[:].bitcast(FP8X4), lhsT_scale=q_sc[:],
+            rhs=kg_w[:].bitcast(FP8X4), rhs_scale=kg_sc[KEYS_ROW:P, :], start=True, stop=True,
+        )
+
+        qg_plain = keep.tile([P, I], U8, name="qg_plain", align_bytes=64)
+        nc.vector.tensor_copy(qg_plain[:], qp_sc[:].indirect(offs_t[:]))
+
+        a_negmax = keep.tile([P, 1], F32, name="a_negmax")
+        a_sum = keep.tile([P, 1], F32, name="a_sum")
+        a_inv = keep.tile([P, 1], F32, name="a_inv")
+        nc.vector.tensor_reduce(out=a_negmax[:], in_=a_ps[:], axis=AXIS_X, op=ALU.max, negate=True)
+        qg_sc = keep.tile([P, I], U8, name="qg_sc", align_bytes=64)
+        nc.vector.tensor_copy(
+            out=qg_sc[:].bitcast(I32).rearrange("p (t m) -> p t m", t=PACK),
+            in_=qg_plain[:].bitcast(I32).rearrange("p (m t) -> p t m", t=PACK),
+        )
+        p_exp = keep.tile([P, I], F32, name="p_exp")
+        nc.scalar.activation(
+            out=p_exp[:].rearrange("q (t m r) -> q t m r", t=PACK, r=RUN),
+            in_=a_ps[:].rearrange("q (m t r) -> q t m r", t=PACK, r=RUN),
+            func=ACT.Exp, bias=a_negmax[:], scale=1.0, accum_out=a_sum[:],
+        )
+
+        qg_w = keep.tile([P, I], U32, name="qg_w", align_bytes=64)
+        nc.vector.tensor_copy(
+            qg_w[:].rearrange("p (t m r) -> p m t r", t=PACK, r=RUN), qp_w[:].indirect(offs_t[:])
+        )
+        nc.vector.reciprocal(out=a_inv[:], in_=a_sum[:])
+        p_norm = keep.tile([P, I], F32, name="p_norm")
+        nc.scalar.activation(out=p_norm[:], in_=p_exp[:], func=ACT.Copy, scale=a_inv[:])
+        wt_ps = psum.tile([P, PACK, Q], F32, name="wt_ps", tag="bank_w")
+        for t in range(PACK):
+            nc.tensor.transpose(wt_ps[:, t, :], p_norm[:, t * P : (t + 1) * P], ident[:])
+
+        k2g_sc = keep.tile([P, J], U8, name="k2g_sc", align_bytes=64)
+        nc.vector.tensor_copy(k2g_sc[:], k2_sc[:].indirect(offs2_t[:]))
+        k2g_w = []
+        for h in range(2):
+            part = keep.tile([P, HALF], U32, name="k2g_w%d" % h, align_bytes=64)
+            nc.vector.tensor_copy(part[:], k2_w[:].indirect(offs2_t[:, h * (HALF // 16) : (h + 1) * (HALF // 16)]))
+            k2g_w.append(part)
+
+        wt_grp = keep.tile([P, Q, PACK], BF16, name="wt_grp", align_bytes=64)
+        for t in range(PACK):
+            nc.scalar.activation(out=wt_grp[:, :, t], in_=wt_ps[:, t, :], func=ACT.Copy, scale=sa_col[:, t : t + 1])
+
+        b_ps = [psum.tile([P, J], F32, name="b_ps%d" % t) for t in range(PACK)]
+        for t in range(PACK):
+            for h in range(2):
+                nc.tensor.matmul_mx(
+                    out=b_ps[t][:, h * HALF : (h + 1) * HALF],
+                    lhsT=qg_w[:, t * P : (t + 1) * P].bitcast(FP8X4), lhsT_scale=qg_sc[QPOOL_ROW:P, t * P : (t + 1) * P],
+                    rhs=k2g_w[h][:].bitcast(FP8X4), rhs_scale=k2g_sc[KEYS2_ROW:P, h * HALF : (h + 1) * HALF],
+                    start=True, stop=True,
+                )
+
+        wt_codes = keep.tile([P, Q], U32, name="wt_codes", align_bytes=64)
+        wt_sc = keep.tile([P, Q], U8, name="wt_sc", align_bytes=64)
+
+        r_exp, b_sum, b_inv = [], [], []
+        for t in range(PACK):
+            negmax = keep.tile([P, 1], F32, name="b_negmax%d" % t)
+            nc.vector.tensor_reduce(out=negmax[:], in_=b_ps[t][:], axis=AXIS_X, op=ALU.max, negate=True)
+            r_exp.append(keep.tile([P, J], F32, name="r_exp%d" % t))
+            b_sum.append(keep.tile([P, 1], F32, name="b_sum%d" % t))
+            b_inv.append(keep.tile([P, 1], F32, name="b_inv%d" % t))
+            nc.scalar.activation(
+                out=r_exp[t][:], in_=b_ps[t][:], func=ACT.Exp, bias=negmax[:], scale=1.0, accum_out=b_sum[t][:]
+            )
+        nc.vector.quantize_mx(out=wt_codes[:].bitcast(FP8X4), scales=wt_sc[:], in_=wt_grp[:].rearrange("p q t -> p (q t)"))
+
+        pairs = [keep.tile([P, 2, HALF, 2], BF16, name="pair%d" % h, align_bytes=64) for h in range(2)]
+        for t in range(PACK):
+            nc.vector.reciprocal(out=b_inv[t][:], in_=b_sum[t][:])
+            for h in range(2):
+                dst, src = pairs[h][:, t // 2, :, t % 2], r_exp[t][:, h * HALF : (h + 1) * HALF]
+                if t >= 2 and h == 1:
+                    factor = keep.tile([P, 1], F32, name="factor%d" % t)
+                    nc.scalar.activation(out=factor[:], in_=b_inv[t][:], func=ACT.Copy, scale=sb_col[:, t : t + 1])
+                    nc.scalar.activation(out=dst, in_=src, func=ACT.Copy, scale=factor[:])
+                else:
+                    nc.vector.tensor_scalar(
+                        out=dst, in0=src, scalar1=b_inv[t][:], scalar2=sb_col[:, t : t + 1], op0=ALU.mult, op1=ALU.mult
+                    )
+        x_grp, x_codes, x_sc = [], [], []
+        for h in range(2):
+            x_grp.append(keep.tile([P, HALF, PACK], BF16, name="x_grp%d" % h, align_bytes=64))
+            x_codes.append(keep.tile([P, HALF], U32, name="x_codes%d" % h, align_bytes=64))
+            x_sc.append(keep.tile([P, HALF], U8, name="x_sc%d" % h, align_bytes=64))
+        for h in range(2):
+            nc.vector.tensor_copy(
+                out=x_grp[h][:].rearrange("p j t -> p (j t)").bitcast(F32).rearrange("p (j u) -> p j u", u=2),
+                in_=pairs[h][:].rearrange("p u j e -> p (u j e)").bitcast(F32).rearrange("p (u j) -> p j u", u=2),
+            )
+        for h in range(2):
+            nc.vector.quantize_mx(
+                out=x_codes[h][:].bitcast(FP8X4), scales=x_sc[h][:], in_=x_grp[h][:].rearrange("p j t -> p (j t)")
+            )
+        for h in range(2):
+            y_ps = psum.tile([P, HALF], F32, name="y_ps%d" % h, tag=("bank_a", "bank_c")[h])
+            nc.tensor.matmul_mx(
+                out=y_ps[:], lhsT=wt_codes[:].bitcast(FP8X4), lhsT_scale=wt_sc[:],
+                rhs=x_codes[h][:].bitcast(FP8X4), rhs_scale=x_sc[h][:], start=True, stop=True,
+            )
+            y_sb = keep.tile([P, HALF], F32, name="y_sb%d" % h)
+            if h == 0:
+                nc.scalar.copy(out=y_sb[:], in_=y_ps[:])
+            else:
+                nc.vector.tensor_copy(out=y_sb[:], in_=y_ps[:])
+            nc.sync.dma_start(out=out[:, h * HALF : (h + 1) * HALF], in_=y_sb[:])

@@ -1,6 +1,7 @@
 from contextlib import ExitStack
 
 import concourse.mybir as mybir
+from concourse.masks import make_identity
 
 F32 = mybir.dt.float32
 BF16 = mybir.dt.bfloat16
@@ -27,11 +28,20 @@ def load_words(nc, tile, words):
     nc.sync.dma_start(out=tile[:].bitcast(I32), in_=words[0].rearrange("p n t -> p (n t)").bitcast(I32))
 
 
-def load_scales(nc, tile, scales, row):
+def load_scales(queue, tile, scales, row, quads=range(4)):
     rows = scales[0].bitcast(I32)
-    for quad in range(4):
+    for quad in quads:
         first = 32 * quad + row
-        nc.sync.dma_start(out=tile[first : first + 4, :].bitcast(I32), in_=rows[4 * quad : 4 * quad + 4, :])
+        queue.dma_start(out=tile[first : first + 4, :].bitcast(I32), in_=rows[4 * quad : 4 * quad + 4, :])
+
+
+def gather_halves(nc, pool, window, offsets, name):
+    halves = []
+    for h in range(2):
+        part = pool.tile([P, HALF], U32, name="%s%d" % (name, h), align_bytes=64)
+        nc.vector.tensor_copy(part[:], window[:].indirect(offsets[:, h * (HALF // 16) : (h + 1) * (HALF // 16)]))
+        halves.append(part)
+    return halves
 
 
 def tile_attend_rollout_kernel(
@@ -45,33 +55,33 @@ def tile_attend_rollout_kernel(
 
         offs_t = keep.tile([P, I // 16], U16, name="offs_t")
         offs2_t = keep.tile([P, J // 16], U16, name="offs2_t")
-        k_sc = keep.tile([P, T], U8, name="k_sc", align_bytes=64)
+        k_sc = keep.tile([P, T], U8, name="k_sc", tag="keys_bytes", align_bytes=64)
         qp_sc = keep.tile([P, T], U8, name="qp_sc", align_bytes=64)
         k2_sc = keep.tile([P, T], U8, name="k2_sc", align_bytes=64)
         ident = keep.tile([P, P], F32, name="ident")
         slot_rows = keep.tile([P, P], F32, name="slot_rows")
 
-        win = 4 * T
-        zeros = big.tile([P, P], F32, name="zeros", offset=win - 256)
-        q_raw = big.tile([P, PACK, Q], F32, name="q_raw", offset=2 * win)
+        q_raw = keep.tile([P, PACK, Q], F32, name="q_raw")
+        k_w = big.tile([P, T], U32, name="k_w", tag="keys_window")
+        qp_w = big.tile([P, T], U32, name="qp_w")
+        k2_w = big.tile([P, T], U32, name="k2_w")
 
-        for plane in (k_sc, qp_sc, k2_sc):
-            nc.vector.memset(plane[:].bitcast(I32), 0)
-        nc.gpsimd.memset(zeros[:], 0.0)
-        nc.gpsimd.affine_select(
-            out=ident[:], in_=zeros[:], compare_op=ALU.not_equal, fill=1.0, base=0, pattern=[[-1, P]], channel_multiplier=1
-        )
+        nc.vector.memset(qp_sc[:, 0 : T // 2].bitcast(I32), 0)
+        nc.gpsimd.memset(qp_sc[:, T // 2 : T].bitcast(I32), 0)
+        nc.vector.memset(k2_sc[:].bitcast(I32), 0)
+        nc.vector.memset(k_sc[:].bitcast(I32), 0)
         nc.gpsimd.memset(slot_rows[:], 0.0)
-
-        k_w = big.tile([P, T], U32, name="k_w", offset=0)
-        qp_w = big.tile([P, T], U32, name="qp_w", offset=win)
+        make_identity(nc, ident[:])
 
         nc.sync.dma_start(offs_t[:], offs)
-        nc.sync.dma_start(out=q_raw[:], in_=query.rearrange("(p j) w -> p j w", j=PACK))
         nc.sync.dma_start(offs2_t[:], offs2)
-        load_scales(nc, k_sc, keys_scales, KEYS_ROW)
+        load_scales(nc.sync, qp_sc, qpool_scales, QPOOL_ROW)
+        load_words(nc, qp_w, qpool_words)
+        load_scales(nc.sync, k2_sc, keys2_scales, KEYS2_ROW)
+        load_words(nc, k2_w, keys2_words)
+        load_scales(nc.sync, k_sc, keys_scales, KEYS_ROW)
+        nc.sync.dma_start(out=q_raw[:], in_=query.rearrange("(p j) w -> p j w", j=PACK))
         load_words(nc, k_w, keys_words)
-        load_scales(nc, qp_sc, qpool_scales, QPOOL_ROW)
         nc.sync.dma_start(
             out=slot_rows[0:PACK, :].rearrange("t (m r) -> t m r", r=RUN),
             in_=sb.rearrange("(m t r) o -> t m (r o)", t=PACK, r=RUN),
@@ -80,76 +90,21 @@ def tile_attend_rollout_kernel(
             out=slot_rows[PACK : 2 * PACK, :].rearrange("t (m r) -> t m r", r=RUN),
             in_=sa.rearrange("o (m t r) -> t (o m) r", t=PACK, r=RUN),
         )
-        load_words(nc, qp_w, qpool_words)
-        load_scales(nc, k2_sc, keys2_scales, KEYS2_ROW)
-
-        q_grp = keep.tile([P, Q, PACK], BF16, name="q_grp", align_bytes=64)
-        nc.scalar.copy(out=q_grp[:], in_=q_raw[:].rearrange("p j w -> p w j"))
-
-        k2_w = big.tile([P, T], U32, name="k2_w", offset=2 * win)
-        load_words(nc, k2_w, keys2_words)
-
-        cols_ps = psum.tile([P, P], F32, name="cols_ps", tag="bank_c")
-        nc.tensor.transpose(cols_ps[:], slot_rows[:], ident[:])
-        sb_col = keep.tile([P, PACK], F32, name="sb_col")
-        sa_col = keep.tile([P, PACK], F32, name="sa_col")
-        nc.scalar.activation(out=sb_col[:], in_=cols_ps[:, 0:PACK], func=ACT.Copy, scale=512.0)
-        nc.scalar.copy(out=sa_col[:], in_=cols_ps[:, PACK : 2 * PACK])
-
-        kg_sc = keep.tile([P, I], U8, name="kg_sc", align_bytes=64)
-        nc.vector.tensor_copy(kg_sc[:], k_sc[:].indirect(offs_t[:]))
-        q_codes = keep.tile([P, Q], U32, name="q_codes", align_bytes=64)
-        q_sc = keep.tile([P, Q], U8, name="q_sc", align_bytes=64)
-        nc.vector.quantize_mx(out=q_codes[:].bitcast(FP8X4), scales=q_sc[:], in_=q_grp[:].rearrange("p w j -> p (w j)"))
-        kg_w = keep.tile([P, I], U32, name="kg_w", align_bytes=64)
-        nc.vector.tensor_copy(kg_w[:], k_w[:].indirect(offs_t[:]))
-        a_ps = psum.tile([P, I], F32, name="a_ps", tag="bank_a")
-        nc.tensor.matmul_mx(
-            out=a_ps[:], lhsT=q_codes[:].bitcast(FP8X4), lhsT_scale=q_sc[:],
-            rhs=kg_w[:].bitcast(FP8X4), rhs_scale=kg_sc[KEYS_ROW:P, :], start=True, stop=True,
-        )
 
         qg_plain = keep.tile([P, I], U8, name="qg_plain", align_bytes=64)
         nc.vector.tensor_copy(qg_plain[:], qp_sc[:].indirect(offs_t[:]))
-
-        a_negmax = keep.tile([P, 1], F32, name="a_negmax")
-        a_sum = keep.tile([P, 1], F32, name="a_sum")
-        a_inv = keep.tile([P, 1], F32, name="a_inv")
-        nc.vector.tensor_reduce(out=a_negmax[:], in_=a_ps[:], axis=AXIS_X, op=ALU.max, negate=True)
+        qg_w = keep.tile([P, I], U32, name="qg_w", align_bytes=64)
+        nc.vector.tensor_copy(
+            qg_w[:].rearrange("p (t m r) -> p m t r", t=PACK, r=RUN), qp_w[:].indirect(offs_t[:])
+        )
         qg_sc = keep.tile([P, I], U8, name="qg_sc", align_bytes=64)
         nc.vector.tensor_copy(
             out=qg_sc[:].bitcast(I32).rearrange("p (t m) -> p t m", t=PACK),
             in_=qg_plain[:].bitcast(I32).rearrange("p (m t) -> p t m", t=PACK),
         )
-        p_exp = keep.tile([P, I], F32, name="p_exp")
-        nc.scalar.activation(
-            out=p_exp[:].rearrange("q (t m r) -> q t m r", t=PACK, r=RUN),
-            in_=a_ps[:].rearrange("q (m t r) -> q t m r", t=PACK, r=RUN),
-            func=ACT.Exp, bias=a_negmax[:], scale=1.0, accum_out=a_sum[:],
-        )
-
-        qg_w = keep.tile([P, I], U32, name="qg_w", align_bytes=64)
-        nc.vector.tensor_copy(
-            qg_w[:].rearrange("p (t m r) -> p m t r", t=PACK, r=RUN), qp_w[:].indirect(offs_t[:])
-        )
-        nc.vector.reciprocal(out=a_inv[:], in_=a_sum[:])
-        p_norm = keep.tile([P, I], F32, name="p_norm")
-        nc.scalar.activation(out=p_norm[:], in_=p_exp[:], func=ACT.Copy, scale=a_inv[:])
-        wt_ps = psum.tile([P, PACK, Q], F32, name="wt_ps", tag="bank_w")
-        for t in range(PACK):
-            nc.tensor.transpose(wt_ps[:, t, :], p_norm[:, t * P : (t + 1) * P], ident[:])
-
         k2g_sc = keep.tile([P, J], U8, name="k2g_sc", align_bytes=64)
         nc.vector.tensor_copy(k2g_sc[:], k2_sc[:].indirect(offs2_t[:]))
-        k2g_w = []
-        for h in range(2):
-            part = keep.tile([P, HALF], U32, name="k2g_w%d" % h, align_bytes=64)
-            nc.vector.tensor_copy(part[:], k2_w[:].indirect(offs2_t[:, h * (HALF // 16) : (h + 1) * (HALF // 16)]))
-            k2g_w.append(part)
-
-        wt_grp = keep.tile([P, Q, PACK], BF16, name="wt_grp", align_bytes=64)
-        for t in range(PACK):
-            nc.scalar.activation(out=wt_grp[:, :, t], in_=wt_ps[:, t, :], func=ACT.Copy, scale=sa_col[:, t : t + 1])
+        k2g_w = gather_halves(nc, keep, k2_w, offs2_t, "k2g_w")
 
         b_ps = [psum.tile([P, J], F32, name="b_ps%d" % t) for t in range(PACK)]
         for t in range(PACK):
@@ -160,34 +115,90 @@ def tile_attend_rollout_kernel(
                     rhs=k2g_w[h][:].bitcast(FP8X4), rhs_scale=k2g_sc[KEYS2_ROW:P, h * HALF : (h + 1) * HALF],
                     start=True, stop=True,
                 )
+        q_grp = keep.tile([P, Q, PACK], BF16, name="q_grp", align_bytes=64)
+        nc.scalar.copy(out=q_grp[:], in_=q_raw[:].rearrange("p j w -> p w j"))
+        q_codes = keep.tile([P, Q], U32, name="q_codes", align_bytes=64)
+        q_sc = keep.tile([P, Q], U8, name="q_sc", align_bytes=64)
+        nc.vector.quantize_mx(out=q_codes[:].bitcast(FP8X4), scales=q_sc[:], in_=q_grp[:].rearrange("p w j -> p (w j)"))
+        kg_sc = keep.tile([P, I], U8, name="kg_sc", align_bytes=64)
+        nc.vector.tensor_copy(kg_sc[:], k_sc[:].indirect(offs_t[:]))
+        kg_w = gather_halves(nc, keep, k_w, offs_t, "kg_w")
+        r_exp = [keep.tile([P, J], F32, name="r_exp%d" % t) for t in range(PACK)]
+        b_sum = keep.tile([P, PACK], F32, name="b_sum")
 
+        def second_softmax(t, negmax):
+            nc.vector.tensor_reduce(out=negmax, in_=b_ps[t][:], axis=AXIS_X, op=ALU.max, negate=True)
+            nc.scalar.activation(
+                out=r_exp[t][:], in_=b_ps[t][:], func=ACT.Exp, bias=negmax, scale=1.0, accum_out=b_sum[:, t : t + 1]
+            )
+
+        early_negmax = keep.tile([P, 2], F32, name="early_negmax", tag="keys_bytes", align_bytes=64)
+        for t in range(2):
+            second_softmax(t, early_negmax[:, t : t + 1])
+
+        cols_ps = psum.tile([P, P], F32, name="cols_ps", tag="bank_c")
+        nc.tensor.transpose(cols_ps[:], slot_rows[:], ident[:])
+        sb_col = keep.tile([P, PACK], F32, name="sb_col")
+        sa_col = keep.tile([P, PACK], F32, name="sa_col")
+        nc.scalar.activation(out=sb_col[:], in_=cols_ps[:, 0:PACK], func=ACT.Copy, scale=512.0)
+        nc.scalar.copy(out=sa_col[:], in_=cols_ps[:, PACK : 2 * PACK])
+        sa_ps = psum.tile([P, PACK, P], F32, name="sa_ps", tag="bank_s")
+        for t in range(PACK):
+            nc.tensor.transpose(sa_ps[:, t, :], sa_col[:, t : t + 1].to_broadcast([P, P]), ident[:])
+
+        a_ps = psum.tile([P, I], F32, name="a_ps", tag="bank_a")
+        for h in range(2):
+            nc.tensor.matmul_mx(
+                out=a_ps[:, h * HALF : (h + 1) * HALF], lhsT=q_codes[:].bitcast(FP8X4), lhsT_scale=q_sc[:],
+                rhs=kg_w[h][:].bitcast(FP8X4), rhs_scale=kg_sc[KEYS_ROW:P, h * HALF : (h + 1) * HALF], start=True, stop=True,
+            )
+        a_negmax = keep.tile([P, 1], F32, name="a_negmax")
+        a_sum = keep.tile([P, 1], F32, name="a_sum")
+        a_inv = keep.tile([P, 1], F32, name="a_inv")
+        nc.vector.tensor_reduce(out=a_negmax[:], in_=a_ps[:], axis=AXIS_X, op=ALU.max, negate=True)
+        p_exp = keep.tile([P, PACK, P], F32, name="p_exp")
+        nc.scalar.activation(
+            out=p_exp[:].rearrange("q t (m r) -> q t m r", r=RUN),
+            in_=a_ps[:].rearrange("q (m t r) -> q t m r", t=PACK, r=RUN),
+            func=ACT.Exp, bias=a_negmax[:], scale=1.0, accum_out=a_sum[:],
+        )
+        late_stats = big.tile([P, 2 + PACK], F32, name="late_stats", tag="keys_window")
+        late_negmax, b_inv = late_stats[:, 0:2], late_stats[:, 2 : 2 + PACK]
+        for t in range(2, PACK):
+            second_softmax(t, late_negmax[:, t - 2 : t - 1])
+        nc.vector.reciprocal(out=a_inv[:], in_=a_sum[:])
+        wt_ps = psum.tile([P, 2, Q], F32, name="wt_ps", tag="bank_w")
+        for u in range(2):
+            w_pair = keep.tile([P, P, 2], BF16, name="w_pair%d" % u, align_bytes=64)
+            nc.vector.scalar_tensor_tensor(
+                out=w_pair[:], in0=p_exp[:, 2 * u : 2 * u + 2, :].rearrange("q e p -> q p e"), scalar=a_inv[:],
+                in1=sa_ps[:, 2 * u : 2 * u + 2, :].rearrange("q e p -> q p e"), op0=ALU.mult, op1=ALU.mult,
+            )
+            nc.tensor.transpose(wt_ps[:, u, :], w_pair[:].rearrange("q p e -> q (p e)").bitcast(F32), ident[:])
+        wt_grp = keep.tile([P, Q, PACK], BF16, name="wt_grp", align_bytes=64)
+        nc.scalar.copy(
+            out=wt_grp[:].rearrange("p q t -> p (q t)").bitcast(F32).rearrange("p (q u) -> p q u", u=2),
+            in_=wt_ps[:].rearrange("p u q -> p q u"),
+        )
         wt_codes = keep.tile([P, Q], U32, name="wt_codes", align_bytes=64)
         wt_sc = keep.tile([P, Q], U8, name="wt_sc", align_bytes=64)
-
-        r_exp, b_sum, b_inv = [], [], []
-        for t in range(PACK):
-            negmax = keep.tile([P, 1], F32, name="b_negmax%d" % t)
-            nc.vector.tensor_reduce(out=negmax[:], in_=b_ps[t][:], axis=AXIS_X, op=ALU.max, negate=True)
-            r_exp.append(keep.tile([P, J], F32, name="r_exp%d" % t))
-            b_sum.append(keep.tile([P, 1], F32, name="b_sum%d" % t))
-            b_inv.append(keep.tile([P, 1], F32, name="b_inv%d" % t))
-            nc.scalar.activation(
-                out=r_exp[t][:], in_=b_ps[t][:], func=ACT.Exp, bias=negmax[:], scale=1.0, accum_out=b_sum[t][:]
-            )
         nc.vector.quantize_mx(out=wt_codes[:].bitcast(FP8X4), scales=wt_sc[:], in_=wt_grp[:].rearrange("p q t -> p (q t)"))
 
         pairs = [keep.tile([P, 2, HALF, 2], BF16, name="pair%d" % h, align_bytes=64) for h in range(2)]
+        factor = keep.tile([P, 2], F32, name="factor")
+        nc.vector.reciprocal(out=b_inv[:, 0:2], in_=b_sum[:, 0:2])
+        for t in range(2):
+            nc.scalar.activation(out=factor[:, t : t + 1], in_=b_inv[:, t : t + 1], func=ACT.Copy, scale=sb_col[:, t : t + 1])
         for t in range(PACK):
-            nc.vector.reciprocal(out=b_inv[t][:], in_=b_sum[t][:])
+            if t >= 2:
+                nc.vector.reciprocal(out=b_inv[:, t : t + 1], in_=b_sum[:, t : t + 1])
             for h in range(2):
                 dst, src = pairs[h][:, t // 2, :, t % 2], r_exp[t][:, h * HALF : (h + 1) * HALF]
-                if t >= 2 and h == 1:
-                    factor = keep.tile([P, 1], F32, name="factor%d" % t)
-                    nc.scalar.activation(out=factor[:], in_=b_inv[t][:], func=ACT.Copy, scale=sb_col[:, t : t + 1])
-                    nc.scalar.activation(out=dst, in_=src, func=ACT.Copy, scale=factor[:])
+                if t < 2:
+                    nc.scalar.activation(out=dst, in_=src, func=ACT.Copy, scale=factor[:, t : t + 1])
                 else:
                     nc.vector.tensor_scalar(
-                        out=dst, in0=src, scalar1=b_inv[t][:], scalar2=sb_col[:, t : t + 1], op0=ALU.mult, op1=ALU.mult
+                        out=dst, in0=src, scalar1=b_inv[:, t : t + 1], scalar2=sb_col[:, t : t + 1], op0=ALU.mult, op1=ALU.mult
                     )
         x_grp, x_codes, x_sc = [], [], []
         for h in range(2):

@@ -59,7 +59,8 @@ def tile_attend_rollout_kernel(
         qp_sc = keep.tile([P, T], U8, name="qp_sc", align_bytes=64)
         k2_sc = keep.tile([P, T], U8, name="k2_sc", align_bytes=64)
         ident = keep.tile([P, P], F32, name="ident")
-        slot_rows = keep.tile([P, P], F32, name="slot_rows")
+        sa_raw = keep.tile([P, RUN], F32, name="sa_raw")
+        sb_raw = keep.tile([P, RUN], F32, name="sb_raw")
 
         q_raw = keep.tile([P, PACK, Q], F32, name="q_raw")
         k_w = big.tile([P, T], U32, name="k_w", tag="keys_window")
@@ -70,26 +71,42 @@ def tile_attend_rollout_kernel(
         nc.gpsimd.memset(qp_sc[:, T // 2 : T].bitcast(I32), 0)
         nc.vector.memset(k2_sc[:].bitcast(I32), 0)
         nc.vector.memset(k_sc[:].bitcast(I32), 0)
-        nc.gpsimd.memset(slot_rows[:], 0.0)
+        nc.gpsimd.dma_start(out=sb_raw[:], in_=sb.rearrange("(p r) o -> p (r o)", r=RUN))
         make_identity(nc, ident[:])
+        minus_one = keep.tile([P, 1], F32, name="minus_one")
+        nc.gpsimd.memset(minus_one[:], -1.0)
+        nc.gpsimd.dma_start(out=sa_raw[:], in_=sa.rearrange("o (p r) -> p (o r)", r=RUN))
 
         nc.sync.dma_start(offs_t[:], offs)
-        nc.sync.dma_start(offs2_t[:], offs2)
+        nc.sync.dma_start(out=q_raw[:], in_=query.rearrange("(p j) w -> p j w", j=PACK))
         load_scales(nc.sync, qp_sc, qpool_scales, QPOOL_ROW)
         load_words(nc, qp_w, qpool_words)
+        nc.sync.dma_start(offs2_t[:], offs2)
         load_scales(nc.sync, k2_sc, keys2_scales, KEYS2_ROW)
         load_words(nc, k2_w, keys2_words)
         load_scales(nc.sync, k_sc, keys_scales, KEYS_ROW)
-        nc.sync.dma_start(out=q_raw[:], in_=query.rearrange("(p j) w -> p j w", j=PACK))
         load_words(nc, k_w, keys_words)
-        nc.sync.dma_start(
-            out=slot_rows[0:PACK, :].rearrange("t (m r) -> t m r", r=RUN),
-            in_=sb.rearrange("(m t r) o -> t m (r o)", t=PACK, r=RUN),
+
+        sb_ps = psum.tile([P, PACK, P], F32, name="sb_ps", tag="bank_w")
+        sa_ps = psum.tile([P, 2, P, 2], F32, name="sa_ps", tag="bank_s")
+        for r in range(RUN):
+            nc.tensor.transpose(
+                sb_ps[:, r, :], sb_raw[:, r : r + 1].to_broadcast([P, P]), ident[:]
+            )
+        for r in range(RUN):
+            nc.tensor.transpose(
+                sa_ps[:].rearrange("q u (m r) e -> q r m u e", r=RUN)[:, r], sa_raw[:, r : r + 1].to_broadcast([P, P]), ident[:]
+            )
+        sb_rows = keep.tile([P, PACK, P], F32, name="sb_rows")
+        nc.scalar.activation(
+            out=sb_rows[:].rearrange("q t (m r) -> q t m r", r=RUN),
+            in_=sb_ps[:].rearrange("q r (m t) -> q t m r", t=PACK), func=ACT.Copy, scale=512.0,
         )
-        nc.sync.dma_start(
-            out=slot_rows[PACK : 2 * PACK, :].rearrange("t (m r) -> t m r", r=RUN),
-            in_=sa.rearrange("o (m t r) -> t (o m) r", t=PACK, r=RUN),
-        )
+        cols_ps = psum.tile([P, PACK, P], F32, name="cols_ps", tag="bank_c")
+        for t in range(PACK):
+            nc.tensor.transpose(cols_ps[:, t, :], sb_rows[:, t, :], ident[:])
+        sb_col = keep.tile([P, PACK], F32, name="sb_col")
+        nc.scalar.copy(out=sb_col[:], in_=cols_ps[:, :, 0])
 
         qg_plain = keep.tile([P, I], U8, name="qg_plain", align_bytes=64)
         nc.vector.tensor_copy(qg_plain[:], qp_sc[:].indirect(offs_t[:]))
@@ -136,16 +153,6 @@ def tile_attend_rollout_kernel(
         for t in range(2):
             second_softmax(t, early_negmax[:, t : t + 1])
 
-        cols_ps = psum.tile([P, P], F32, name="cols_ps", tag="bank_c")
-        nc.tensor.transpose(cols_ps[:], slot_rows[:], ident[:])
-        sb_col = keep.tile([P, PACK], F32, name="sb_col")
-        sa_col = keep.tile([P, PACK], F32, name="sa_col")
-        nc.scalar.activation(out=sb_col[:], in_=cols_ps[:, 0:PACK], func=ACT.Copy, scale=512.0)
-        nc.scalar.copy(out=sa_col[:], in_=cols_ps[:, PACK : 2 * PACK])
-        sa_ps = psum.tile([P, PACK, P], F32, name="sa_ps", tag="bank_s")
-        for t in range(PACK):
-            nc.tensor.transpose(sa_ps[:, t, :], sa_col[:, t : t + 1].to_broadcast([P, P]), ident[:])
-
         a_ps = psum.tile([P, I], F32, name="a_ps", tag="bank_a")
         for h in range(2):
             nc.tensor.matmul_mx(
@@ -166,13 +173,17 @@ def tile_attend_rollout_kernel(
         late_negmax, b_inv = late_stats[:, 0:2], late_stats[:, 2 : 2 + PACK]
         for t in range(2, PACK):
             second_softmax(t, late_negmax[:, t - 2 : t - 1])
+        first_inv = keep.tile([P, 1], F32, name="first_inv")
         nc.vector.reciprocal(out=a_inv[:], in_=a_sum[:])
+        nc.gpsimd.tensor_tensor(out=first_inv[:], in0=b_sum[:, 0:1], in1=minus_one[:], op=ALU.pow)
+        nc.vector.reciprocal(out=b_inv[:, 1:3], in_=b_sum[:, 1:3])
+        nc.vector.reciprocal(out=b_inv[:, 3:4], in_=b_sum[:, 3:4])
         wt_ps = psum.tile([P, 2, Q], F32, name="wt_ps", tag="bank_w")
         for u in range(2):
             w_pair = keep.tile([P, P, 2], BF16, name="w_pair%d" % u, align_bytes=64)
             nc.vector.scalar_tensor_tensor(
                 out=w_pair[:], in0=p_exp[:, 2 * u : 2 * u + 2, :].rearrange("q e p -> q p e"), scalar=a_inv[:],
-                in1=sa_ps[:, 2 * u : 2 * u + 2, :].rearrange("q e p -> q p e"), op0=ALU.mult, op1=ALU.mult,
+                in1=sa_ps[:, u, :, :], op0=ALU.mult, op1=ALU.mult,
             )
             nc.tensor.transpose(wt_ps[:, u, :], w_pair[:].rearrange("q p e -> q (p e)").bitcast(F32), ident[:])
         wt_grp = keep.tile([P, Q, PACK], BF16, name="wt_grp", align_bytes=64)
@@ -182,24 +193,24 @@ def tile_attend_rollout_kernel(
         )
         wt_codes = keep.tile([P, Q], U32, name="wt_codes", align_bytes=64)
         wt_sc = keep.tile([P, Q], U8, name="wt_sc", align_bytes=64)
-        nc.vector.quantize_mx(out=wt_codes[:].bitcast(FP8X4), scales=wt_sc[:], in_=wt_grp[:].rearrange("p q t -> p (q t)"))
 
-        pairs = [keep.tile([P, 2, HALF, 2], BF16, name="pair%d" % h, align_bytes=64) for h in range(2)]
+        pairs = keep.tile([P, 2, 2, HALF, 2], BF16, name="pairs", align_bytes=64)
         factor = keep.tile([P, 2], F32, name="factor")
-        nc.vector.reciprocal(out=b_inv[:, 0:2], in_=b_sum[:, 0:2])
         for t in range(2):
-            nc.scalar.activation(out=factor[:, t : t + 1], in_=b_inv[:, t : t + 1], func=ACT.Copy, scale=sb_col[:, t : t + 1])
-        for t in range(PACK):
-            if t >= 2:
-                nc.vector.reciprocal(out=b_inv[:, t : t + 1], in_=b_sum[:, t : t + 1])
-            for h in range(2):
-                dst, src = pairs[h][:, t // 2, :, t % 2], r_exp[t][:, h * HALF : (h + 1) * HALF]
-                if t < 2:
-                    nc.scalar.activation(out=dst, in_=src, func=ACT.Copy, scale=factor[:, t : t + 1])
-                else:
-                    nc.vector.tensor_scalar(
-                        out=dst, in0=src, scalar1=b_inv[:, t : t + 1], scalar2=sb_col[:, t : t + 1], op0=ALU.mult, op1=ALU.mult
-                    )
+            inv = first_inv[:] if t == 0 else b_inv[:, t : t + 1]
+            nc.scalar.activation(out=factor[:, t : t + 1], in_=inv, func=ACT.Copy, scale=sb_col[:, t : t + 1])
+            nc.scalar.activation(
+                out=pairs[:, :, 0, :, t], in_=r_exp[t][:].rearrange("p (h j) -> p h j", h=2), func=ACT.Copy, scale=factor[:, t : t + 1]
+            )
+        nc.vector.tensor_scalar(
+            out=pairs[:, :, 1, :, 0], in0=r_exp[2][:].rearrange("p (h j) -> p h j", h=2),
+            scalar1=b_inv[:, 2:3], scalar2=sb_col[:, 2:3], op0=ALU.mult, op1=ALU.mult,
+        )
+        for h in range(2):
+            nc.vector.tensor_scalar(
+                out=pairs[:, h, 1, :, 1], in0=r_exp[3][:, h * HALF : (h + 1) * HALF],
+                scalar1=b_inv[:, 3:4], scalar2=sb_col[:, 3:4], op0=ALU.mult, op1=ALU.mult,
+            )
         x_grp, x_codes, x_sc = [], [], []
         for h in range(2):
             x_grp.append(keep.tile([P, HALF, PACK], BF16, name="x_grp%d" % h, align_bytes=64))
@@ -208,12 +219,16 @@ def tile_attend_rollout_kernel(
         for h in range(2):
             nc.vector.tensor_copy(
                 out=x_grp[h][:].rearrange("p j t -> p (j t)").bitcast(F32).rearrange("p (j u) -> p j u", u=2),
-                in_=pairs[h][:].rearrange("p u j e -> p (u j e)").bitcast(F32).rearrange("p (u j) -> p j u", u=2),
+                in_=pairs[:, h].rearrange("p u j e -> p (u j e)").bitcast(F32).rearrange("p (u j) -> p j u", u=2),
             )
         for h in range(2):
             nc.vector.quantize_mx(
                 out=x_codes[h][:].bitcast(FP8X4), scales=x_sc[h][:], in_=x_grp[h][:].rearrange("p j t -> p (j t)")
             )
+            if h == 0:
+                nc.vector.quantize_mx(
+                    out=wt_codes[:].bitcast(FP8X4), scales=wt_sc[:], in_=wt_grp[:].rearrange("p q t -> p (q t)")
+                )
         for h in range(2):
             y_ps = psum.tile([P, HALF], F32, name="y_ps%d" % h, tag=("bank_a", "bank_c")[h])
             nc.tensor.matmul_mx(

@@ -21,18 +21,22 @@ HALF = J // 2
 RUN = 4
 FLOPS = 2 * D * Q * I + 2 * D * I * J + 2 * I * Q * J
 
-KEYS_ROW, QPOOL_ROW, KEYS2_ROW = 0, 8, 4
+SCALE_ROWS = 16
 
 
 def load_words(nc, tile, words):
     nc.sync.dma_start(out=tile[:].bitcast(I32), in_=words[0].rearrange("p n t -> p (n t)").bitcast(I32))
 
 
-def load_scales(queue, tile, scales, row, quads=range(4)):
-    rows = scales[0].bitcast(I32)
-    for quad in quads:
-        first = 32 * quad + row
-        queue.dma_start(out=tile[first : first + 4, :].bitcast(I32), in_=rows[4 * quad : 4 * quad + 4, :])
+def load_scales(nc, tile, scales, first_row=0, rows=SCALE_ROWS, partition=0):
+    nc.sync.dma_start(
+        out=tile[partition : partition + rows, :].bitcast(I32), in_=scales[0].bitcast(I32)[first_row : first_row + rows, :]
+    )
+
+
+def place_scale_rows(queue, plane, source, moves):
+    for quad, row in moves:
+        queue.dma_start(out=plane[32 * quad : 32 * quad + 4, :].bitcast(I32), in_=source[row : row + 4, :].bitcast(I32))
 
 
 def gather_halves(nc, pool, window, offsets, name):
@@ -55,7 +59,7 @@ def tile_attend_rollout_kernel(
 
         offs_t = keep.tile([P, I // 16], U16, name="offs_t")
         offs2_t = keep.tile([P, J // 16], U16, name="offs2_t")
-        k_sc = keep.tile([P, T], U8, name="k_sc", tag="keys_bytes", align_bytes=64)
+        k_sc = keep.tile([P, T], U8, name="k_sc", align_bytes=64)
         qp_sc = keep.tile([P, T], U8, name="qp_sc", align_bytes=64)
         k2_sc = keep.tile([P, T], U8, name="k2_sc", align_bytes=64)
         ident = keep.tile([P, P], F32, name="ident")
@@ -63,13 +67,12 @@ def tile_attend_rollout_kernel(
         sb_raw = keep.tile([P, RUN], F32, name="sb_raw")
 
         q_raw = keep.tile([P, PACK, Q], F32, name="q_raw")
-        k_w = big.tile([P, T], U32, name="k_w", tag="keys_window")
         qp_w = big.tile([P, T], U32, name="qp_w")
-        k2_w = big.tile([P, T], U32, name="k2_w")
+        k2_w = big.tile([P, T], U32, name="k2_w", tag="keys2_window", align_bytes=64)
 
-        nc.vector.memset(qp_sc[:, 0 : T // 2].bitcast(I32), 0)
-        nc.gpsimd.memset(qp_sc[:, T // 2 : T].bitcast(I32), 0)
-        nc.vector.memset(k2_sc[:].bitcast(I32), 0)
+        for plane in (qp_sc, k2_sc):
+            nc.vector.memset(plane[:, 0 : T // 2].bitcast(I32), 0)
+            nc.gpsimd.memset(plane[:, T // 2 : T].bitcast(I32), 0)
         nc.vector.memset(k_sc[:].bitcast(I32), 0)
         nc.gpsimd.dma_start(out=sb_raw[:], in_=sb.rearrange("(p r) o -> p (r o)", r=RUN))
         make_identity(nc, ident[:])
@@ -78,14 +81,15 @@ def tile_attend_rollout_kernel(
         nc.gpsimd.dma_start(out=sa_raw[:], in_=sa.rearrange("o (p r) -> p (o r)", r=RUN))
 
         nc.sync.dma_start(offs_t[:], offs)
-        nc.sync.dma_start(out=q_raw[:], in_=query.rearrange("(p j) w -> p j w", j=PACK))
-        load_scales(nc.sync, qp_sc, qpool_scales, QPOOL_ROW)
-        load_words(nc, qp_w, qpool_words)
         nc.sync.dma_start(offs2_t[:], offs2)
-        load_scales(nc.sync, k2_sc, keys2_scales, KEYS2_ROW)
+        load_scales(nc, qp_sc, qpool_scales, 0, 8, 0)
+        load_scales(nc, qp_sc, qpool_scales, 8, 8, 64)
+        load_scales(nc, k2_sc, keys2_scales)
+        load_words(nc, qp_w, qpool_words)
+        for quad in range(4):
+            load_scales(nc, k_sc, keys_scales, 4 * quad, 4, 32 * quad)
         load_words(nc, k2_w, keys2_words)
-        load_scales(nc.sync, k_sc, keys_scales, KEYS_ROW)
-        load_words(nc, k_w, keys_words)
+        nc.sync.dma_start(out=q_raw[:], in_=query.rearrange("(p j) w -> p j w", j=PACK))
 
         sb_ps = psum.tile([P, PACK, P], F32, name="sb_ps", tag="bank_w")
         sa_ps = psum.tile([P, 2, P, 2], F32, name="sa_ps", tag="bank_s")
@@ -110,17 +114,25 @@ def tile_attend_rollout_kernel(
 
         qg_plain = keep.tile([P, I], U8, name="qg_plain", align_bytes=64)
         nc.vector.tensor_copy(qg_plain[:], qp_sc[:].indirect(offs_t[:]))
-        qg_w = keep.tile([P, I], U32, name="qg_w", align_bytes=64)
-        nc.vector.tensor_copy(
-            qg_w[:].rearrange("p (t m r) -> p m t r", t=PACK, r=RUN), qp_w[:].indirect(offs_t[:])
-        )
         qg_sc = keep.tile([P, I], U8, name="qg_sc", align_bytes=64)
         nc.vector.tensor_copy(
             out=qg_sc[:].bitcast(I32).rearrange("p (t m) -> p t m", t=PACK),
             in_=qg_plain[:].bitcast(I32).rearrange("p (m t) -> p t m", t=PACK),
         )
+        place_scale_rows(nc.sync, qg_sc, qg_sc, ((1, 4), (3, 68)))
+        k2g_plain = big.tile([P, J], U8, name="k2g_plain", tag="keys_window", align_bytes=64)
+        nc.vector.tensor_copy(k2g_plain[:], k2_sc[:].indirect(offs2_t[:]))
         k2g_sc = keep.tile([P, J], U8, name="k2g_sc", align_bytes=64)
-        nc.vector.tensor_copy(k2g_sc[:], k2_sc[:].indirect(offs2_t[:]))
+        nc.vector.tensor_copy(out=k2g_sc[:].bitcast(I32), in_=k2g_plain[:].bitcast(I32))
+        place_scale_rows(nc.sync, k2g_sc, k2g_sc, ((1, 4), (2, 8), (3, 12)))
+        k_w = big.tile([P, T], U32, name="k_w", tag="keys_window", align_bytes=64)
+        load_words(nc, k_w, keys_words)
+        qg_w = keep.tile([P, I], U32, name="qg_w", align_bytes=64)
+        nc.vector.tensor_copy(
+            qg_w[:].rearrange("p (t m r) -> p m t r", t=PACK, r=RUN), qp_w[:].indirect(offs_t[:])
+        )
+        kg_sc = keep.tile([P, I], U8, name="kg_sc", align_bytes=64)
+        nc.vector.tensor_copy(kg_sc[:], k_sc[:].indirect(offs_t[:]))
         k2g_w = gather_halves(nc, keep, k2_w, offs2_t, "k2g_w")
 
         b_ps = [psum.tile([P, J], F32, name="b_ps%d" % t) for t in range(PACK)]
@@ -128,17 +140,15 @@ def tile_attend_rollout_kernel(
             for h in range(2):
                 nc.tensor.matmul_mx(
                     out=b_ps[t][:, h * HALF : (h + 1) * HALF],
-                    lhsT=qg_w[:, t * P : (t + 1) * P].bitcast(FP8X4), lhsT_scale=qg_sc[QPOOL_ROW:P, t * P : (t + 1) * P],
-                    rhs=k2g_w[h][:].bitcast(FP8X4), rhs_scale=k2g_sc[KEYS2_ROW:P, h * HALF : (h + 1) * HALF],
+                    lhsT=qg_w[:, t * P : (t + 1) * P].bitcast(FP8X4), lhsT_scale=qg_sc[:, t * P : (t + 1) * P],
+                    rhs=k2g_w[h][:].bitcast(FP8X4), rhs_scale=k2g_sc[:, h * HALF : (h + 1) * HALF],
                     start=True, stop=True,
                 )
         q_grp = keep.tile([P, Q, PACK], BF16, name="q_grp", align_bytes=64)
         nc.scalar.copy(out=q_grp[:], in_=q_raw[:].rearrange("p j w -> p w j"))
         q_codes = keep.tile([P, Q], U32, name="q_codes", align_bytes=64)
-        q_sc = keep.tile([P, Q], U8, name="q_sc", align_bytes=64)
+        q_sc = big.tile([P, Q], U8, name="q_sc", tag="keys2_window", align_bytes=64)
         nc.vector.quantize_mx(out=q_codes[:].bitcast(FP8X4), scales=q_sc[:], in_=q_grp[:].rearrange("p w j -> p (w j)"))
-        kg_sc = keep.tile([P, I], U8, name="kg_sc", align_bytes=64)
-        nc.vector.tensor_copy(kg_sc[:], k_sc[:].indirect(offs_t[:]))
         kg_w = gather_halves(nc, keep, k_w, offs_t, "kg_w")
         r_exp = [keep.tile([P, J], F32, name="r_exp%d" % t) for t in range(PACK)]
         b_sum = keep.tile([P, PACK], F32, name="b_sum")
@@ -149,7 +159,7 @@ def tile_attend_rollout_kernel(
                 out=r_exp[t][:], in_=b_ps[t][:], func=ACT.Exp, bias=negmax, scale=1.0, accum_out=b_sum[:, t : t + 1]
             )
 
-        early_negmax = keep.tile([P, 2], F32, name="early_negmax", tag="keys_bytes", align_bytes=64)
+        early_negmax = keep.tile([P, 2], F32, name="early_negmax")
         for t in range(2):
             second_softmax(t, early_negmax[:, t : t + 1])
 
@@ -157,7 +167,7 @@ def tile_attend_rollout_kernel(
         for h in range(2):
             nc.tensor.matmul_mx(
                 out=a_ps[:, h * HALF : (h + 1) * HALF], lhsT=q_codes[:].bitcast(FP8X4), lhsT_scale=q_sc[:],
-                rhs=kg_w[h][:].bitcast(FP8X4), rhs_scale=kg_sc[KEYS_ROW:P, h * HALF : (h + 1) * HALF], start=True, stop=True,
+                rhs=kg_w[h][:].bitcast(FP8X4), rhs_scale=kg_sc[:, h * HALF : (h + 1) * HALF], start=True, stop=True,
             )
         a_negmax = keep.tile([P, 1], F32, name="a_negmax")
         a_sum = keep.tile([P, 1], F32, name="a_sum")
@@ -169,7 +179,7 @@ def tile_attend_rollout_kernel(
             in_=a_ps[:].rearrange("q (m t r) -> q t m r", t=PACK, r=RUN),
             func=ACT.Exp, bias=a_negmax[:], scale=1.0, accum_out=a_sum[:],
         )
-        late_stats = big.tile([P, 2 + PACK], F32, name="late_stats", tag="keys_window")
+        late_stats = big.tile([P, 2 + PACK], F32, name="late_stats", tag="keys_window", align_bytes=64)
         late_negmax, b_inv = late_stats[:, 0:2], late_stats[:, 2 : 2 + PACK]
         for t in range(2, PACK):
             second_softmax(t, late_negmax[:, t - 2 : t - 1])

@@ -22,6 +22,7 @@ RUN = 4
 FLOPS = 2 * D * Q * I + 2 * D * I * J + 2 * I * Q * J
 
 SCALE_ROWS = 16
+ROW_STEP = 8
 
 
 def load_words(nc, tile, words):
@@ -34,6 +35,15 @@ def load_scales(nc, tile, scales, first_row=0, rows=SCALE_ROWS, partition=0):
     )
 
 
+def load_spread_scales(nc, tile, scales):
+    nc.sync.dma_start(out=tile[0:P:ROW_STEP, :].bitcast(I32), in_=scales[0].bitcast(I32))
+
+
+def place_spread_rows(nc, plane, source, first):
+    for r in range(first, 4):
+        nc.sync.dma_start(out=plane[r:P:32, :].bitcast(I32), in_=source[ROW_STEP * r : P : 32, :].bitcast(I32))
+
+
 def place_scale_rows(queue, plane, source, moves):
     for quad, row in moves:
         queue.dma_start(out=plane[32 * quad : 32 * quad + 4, :].bitcast(I32), in_=source[row : row + 4, :].bitcast(I32))
@@ -42,7 +52,7 @@ def place_scale_rows(queue, plane, source, moves):
 def gather_halves(nc, pool, window, offsets, name):
     halves = []
     for h in range(2):
-        part = pool.tile([P, HALF], U32, name="%s%d" % (name, h), align_bytes=64)
+        part = pool.tile([P, HALF], U32, name="%s%d" % (name, h), tag="%s%d" % (name, h), align_bytes=64)
         nc.vector.tensor_copy(part[:], window[:].indirect(offsets[:, h * (HALF // 16) : (h + 1) * (HALF // 16)]))
         halves.append(part)
     return halves
@@ -74,7 +84,8 @@ def tile_attend_rollout_kernel(
             nc.vector.memset(plane[:, 0 : T // 2].bitcast(I32), 0)
             nc.gpsimd.memset(plane[:, T // 2 : T].bitcast(I32), 0)
         nc.vector.memset(k_sc[:].bitcast(I32), 0)
-        nc.gpsimd.dma_start(out=sb_raw[:], in_=sb.rearrange("(p r) o -> p (r o)", r=RUN))
+        kg_sc = keep.tile([P, I], U8, name="kg_sc", align_bytes=64)
+        nc.vector.memset(kg_sc[:].bitcast(I32), 0)
         make_identity(nc, ident[:])
         minus_one = keep.tile([P, 1], F32, name="minus_one")
         nc.gpsimd.memset(minus_one[:], -1.0)
@@ -84,10 +95,10 @@ def tile_attend_rollout_kernel(
         nc.sync.dma_start(offs2_t[:], offs2)
         load_scales(nc, qp_sc, qpool_scales, 0, 8, 0)
         load_scales(nc, qp_sc, qpool_scales, 8, 8, 64)
-        load_scales(nc, k2_sc, keys2_scales)
+        load_spread_scales(nc, k2_sc, keys2_scales)
         load_words(nc, qp_w, qpool_words)
-        for quad in range(4):
-            load_scales(nc, k_sc, keys_scales, 4 * quad, 4, 32 * quad)
+        load_spread_scales(nc, k_sc, keys_scales)
+        nc.sync.dma_start(out=sb_raw[:], in_=sb.rearrange("(p r) o -> p (r o)", r=RUN))
         load_words(nc, k2_w, keys2_words)
         nc.sync.dma_start(out=q_raw[:], in_=query.rearrange("(p j) w -> p j w", j=PACK))
 
@@ -124,15 +135,16 @@ def tile_attend_rollout_kernel(
         nc.vector.tensor_copy(k2g_plain[:], k2_sc[:].indirect(offs2_t[:]))
         k2g_sc = keep.tile([P, J], U8, name="k2g_sc", align_bytes=64)
         nc.vector.tensor_copy(out=k2g_sc[:].bitcast(I32), in_=k2g_plain[:].bitcast(I32))
-        place_scale_rows(nc.sync, k2g_sc, k2g_sc, ((1, 4), (2, 8), (3, 12)))
+        place_spread_rows(nc, k2g_sc, k2g_sc, 1)
         k_w = big.tile([P, T], U32, name="k_w", tag="keys_window", align_bytes=64)
         load_words(nc, k_w, keys_words)
         qg_w = keep.tile([P, I], U32, name="qg_w", align_bytes=64)
         nc.vector.tensor_copy(
             qg_w[:].rearrange("p (t m r) -> p m t r", t=PACK, r=RUN), qp_w[:].indirect(offs_t[:])
         )
-        kg_sc = keep.tile([P, I], U8, name="kg_sc", align_bytes=64)
-        nc.vector.tensor_copy(kg_sc[:], k_sc[:].indirect(offs_t[:]))
+        kg_plain = keep.tile([P, I], U8, name="kg_plain", align_bytes=64)
+        nc.vector.tensor_copy(kg_plain[:], k_sc[:].indirect(offs_t[:]))
+        place_spread_rows(nc, kg_sc, kg_plain, 0)
         k2g_w = gather_halves(nc, keep, k2_w, offs2_t, "k2g_w")
 
         b_ps = [psum.tile([P, J], F32, name="b_ps%d" % t) for t in range(PACK)]
@@ -179,10 +191,11 @@ def tile_attend_rollout_kernel(
             in_=a_ps[:].rearrange("q (m t r) -> q t m r", t=PACK, r=RUN),
             func=ACT.Exp, bias=a_negmax[:], scale=1.0, accum_out=a_sum[:],
         )
-        late_stats = big.tile([P, 2 + PACK], F32, name="late_stats", tag="keys_window", align_bytes=64)
-        late_negmax, b_inv = late_stats[:, 0:2], late_stats[:, 2 : 2 + PACK]
-        for t in range(2, PACK):
-            second_softmax(t, late_negmax[:, t - 2 : t - 1])
+        third_negmax = big.tile([P, 1], F32, name="third_negmax", tag="keys_window", align_bytes=64)
+        second_softmax(2, third_negmax[:])
+        late_stats = keep.tile([P, 1 + PACK], F32, name="late_stats", tag="kg_w1", align_bytes=64)
+        b_inv = late_stats[:, 1 : 1 + PACK]
+        second_softmax(3, late_stats[:, 0:1])
         first_inv = keep.tile([P, 1], F32, name="first_inv")
         nc.vector.reciprocal(out=a_inv[:], in_=a_sum[:])
         nc.gpsimd.tensor_tensor(out=first_inv[:], in0=b_sum[:, 0:1], in1=minus_one[:], op=ALU.pow)

@@ -142,10 +142,13 @@ def tile_attend_rollout_kernel(
         nc.vector.tensor_copy(
             qg_w[:].rearrange("p (t m r) -> p m t r", t=PACK, r=RUN), qp_w[:].indirect(offs_t[:])
         )
-        kg_plain = keep.tile([P, I], U8, name="kg_plain", align_bytes=64)
-        nc.vector.tensor_copy(kg_plain[:], k_sc[:].indirect(offs_t[:]))
-        place_spread_rows(nc, kg_sc, kg_plain, 0)
+        kg_first = keep.tile([P, HALF], U8, name="kg_first", align_bytes=64)
+        nc.vector.tensor_copy(kg_first[:], k_sc[:].indirect(offs_t[:, 0 : HALF // 16]))
+        place_spread_rows(nc, kg_sc[:, 0:HALF], kg_first, 0)
         k2g_w = gather_halves(nc, keep, k2_w, offs2_t, "k2g_w")
+        kg_second = big.tile([P, HALF], U8, name="kg_second", tag="keys2_window", align_bytes=64)
+        nc.vector.tensor_copy(kg_second[:], k_sc[:].indirect(offs_t[:, HALF // 16 : I // 16]))
+        place_spread_rows(nc, kg_sc[:, HALF:I], kg_second, 0)
 
         b_ps = [psum.tile([P, J], F32, name="b_ps%d" % t) for t in range(PACK)]
         for t in range(PACK):
@@ -159,7 +162,7 @@ def tile_attend_rollout_kernel(
         q_grp = keep.tile([P, Q, PACK], BF16, name="q_grp", align_bytes=64)
         nc.scalar.copy(out=q_grp[:], in_=q_raw[:].rearrange("p j w -> p w j"))
         q_codes = keep.tile([P, Q], U32, name="q_codes", align_bytes=64)
-        q_sc = big.tile([P, Q], U8, name="q_sc", tag="keys2_window", align_bytes=64)
+        q_sc = keep.tile([P, Q], U8, name="q_sc", align_bytes=64)
         nc.vector.quantize_mx(out=q_codes[:].bitcast(FP8X4), scales=q_sc[:], in_=q_grp[:].rearrange("p w j -> p (w j)"))
         kg_w = gather_halves(nc, keep, k_w, offs_t, "kg_w")
         r_exp = [keep.tile([P, J], F32, name="r_exp%d" % t) for t in range(PACK)]
@@ -218,12 +221,15 @@ def tile_attend_rollout_kernel(
         wt_sc = keep.tile([P, Q], U8, name="wt_sc", align_bytes=64)
 
         pairs = keep.tile([P, 2, 2, HALF, 2], BF16, name="pairs", align_bytes=64)
-        factor = keep.tile([P, 2], F32, name="factor")
         for t in range(2):
             inv = first_inv[:] if t == 0 else b_inv[:, t : t + 1]
-            nc.scalar.activation(out=factor[:, t : t + 1], in_=inv, func=ACT.Copy, scale=sb_col[:, t : t + 1])
+            factor = keep.tile([P, 1], F32, name="factor%d" % t)
+            if t == 0:
+                nc.scalar.activation(out=factor[:], in_=inv, func=ACT.Copy, scale=sb_col[:, t : t + 1])
+            else:
+                nc.gpsimd.tensor_tensor(out=factor[:], in0=inv, in1=sb_col[:, t : t + 1], op=ALU.mult)
             nc.scalar.activation(
-                out=pairs[:, :, 0, :, t], in_=r_exp[t][:].rearrange("p (h j) -> p h j", h=2), func=ACT.Copy, scale=factor[:, t : t + 1]
+                out=pairs[:, :, 0, :, t], in_=r_exp[t][:].rearrange("p (h j) -> p h j", h=2), func=ACT.Copy, scale=factor[:]
             )
         nc.vector.tensor_scalar(
             out=pairs[:, :, 1, :, 0], in0=r_exp[2][:].rearrange("p (h j) -> p h j", h=2),

@@ -73,8 +73,7 @@ def tile_attend_rollout_kernel(
         qp_sc = keep.tile([P, T], U8, name="qp_sc", align_bytes=64)
         k2_sc = keep.tile([P, T], U8, name="k2_sc", align_bytes=64)
         ident = keep.tile([P, P], F32, name="ident")
-        sa_raw = keep.tile([P, RUN], F32, name="sa_raw")
-        sb_raw = keep.tile([P, RUN], F32, name="sb_raw")
+        sb_raw = keep.tile([P, RUN], F32, name="sb_raw", tag="slot_weights")
 
         q_raw = keep.tile([P, PACK, Q], F32, name="q_raw")
         qp_w = big.tile([P, T], U32, name="qp_w")
@@ -89,7 +88,6 @@ def tile_attend_rollout_kernel(
         make_identity(nc, ident[:])
         minus_one = keep.tile([P, 1], F32, name="minus_one")
         nc.gpsimd.memset(minus_one[:], -1.0)
-        nc.gpsimd.dma_start(out=sa_raw[:], in_=sa.rearrange("o (p r) -> p (o r)", r=RUN))
 
         nc.sync.dma_start(offs_t[:], offs)
         nc.sync.dma_start(offs2_t[:], offs2)
@@ -107,10 +105,6 @@ def tile_attend_rollout_kernel(
         for r in range(RUN):
             nc.tensor.transpose(
                 sb_ps[:, r, :], sb_raw[:, r : r + 1].to_broadcast([P, P]), ident[:]
-            )
-        for r in range(RUN):
-            nc.tensor.transpose(
-                sa_ps[:].rearrange("q u (m r) e -> q r m u e", r=RUN)[:, r], sa_raw[:, r : r + 1].to_broadcast([P, P]), ident[:]
             )
         sb_rows = keep.tile([P, PACK, P], F32, name="sb_rows")
         nc.scalar.activation(
@@ -174,6 +168,12 @@ def tile_attend_rollout_kernel(
                 out=r_exp[t][:], in_=b_ps[t][:], func=ACT.Exp, bias=negmax, scale=1.0, accum_out=b_sum[:, t : t + 1]
             )
 
+        sa_raw = keep.tile([P, RUN], F32, name="sa_raw", tag="slot_weights")
+        nc.sync.dma_start(out=sa_raw[:], in_=sa.rearrange("o (p r) -> p (o r)", r=RUN))
+        for r in range(RUN):
+            nc.tensor.transpose(
+                sa_ps[:].rearrange("q u (m r) e -> q r m u e", r=RUN)[:, r], sa_raw[:, r : r + 1].to_broadcast([P, P]), ident[:]
+            )
         early_negmax = keep.tile([P, 2], F32, name="early_negmax")
         for t in range(2):
             second_softmax(t, early_negmax[:, t : t + 1])

@@ -79,29 +79,30 @@ def tile_attend_rollout_kernel(
         qp_w = big.tile([P, T], U32, name="qp_w")
         k2_w = big.tile([P, T], U32, name="k2_w", tag="keys2_window", align_bytes=64)
 
-        for plane in (qp_sc, k2_sc):
-            nc.vector.memset(plane[:, 0 : T // 2].bitcast(I32), 0)
-            nc.gpsimd.memset(plane[:, T // 2 : T].bitcast(I32), 0)
+        nc.vector.memset(k2_sc[:, 0 : T // 2].bitcast(I32), 0)
+        nc.gpsimd.memset(k2_sc[:, T // 2 : T].bitcast(I32), 0)
+        nc.vector.memset(qp_sc[64:P, :].bitcast(I32), 0)
+        nc.gpsimd.memset(qp_sc[32:64, :].bitcast(I32), 0)
         nc.vector.memset(k_sc[:].bitcast(I32), 0)
-        kg_sc = keep.tile([P, I], U8, name="kg_sc", align_bytes=64)
-        nc.vector.memset(kg_sc[:].bitcast(I32), 0)
+        kg_sc = [keep.tile([P, HALF], U8, name="kg_sc%d" % h, align_bytes=64) for h in range(2)]
+        nc.vector.memset(kg_sc[1][:].bitcast(I32), 0)
         make_identity(nc, ident[:])
         minus_one = keep.tile([P, 1], F32, name="minus_one")
         nc.gpsimd.memset(minus_one[:], -1.0)
 
         nc.sync.dma_start(offs_t[:], offs)
+        load_scales(nc, qp_sc, qpool_scales, 0, SCALE_ROWS, 0)
+        load_scales(nc, qp_sc, qpool_scales, 0, SCALE_ROWS, SCALE_ROWS)
         nc.sync.dma_start(offs2_t[:], offs2)
-        load_scales(nc, qp_sc, qpool_scales, 0, 8, 0)
-        load_scales(nc, qp_sc, qpool_scales, 8, 8, 64)
-        load_spread_scales(nc, k2_sc, keys2_scales)
+        nc.sync.dma_start(out=sb_raw[:], in_=sb.rearrange("(p r) o -> p (r o)", r=RUN))
+        load_scales(nc, k2_sc, keys2_scales, 0, 8, 0)
+        load_scales(nc, k2_sc, keys2_scales, 8, 8, 64)
         load_words(nc, qp_w, qpool_words)
         load_spread_scales(nc, k_sc, keys_scales)
-        nc.sync.dma_start(out=sb_raw[:], in_=sb.rearrange("(p r) o -> p (r o)", r=RUN))
         load_words(nc, k2_w, keys2_words)
         nc.sync.dma_start(out=q_raw[:], in_=query.rearrange("(p j) w -> p j w", j=PACK))
 
         sb_ps = psum.tile([P, PACK, P], F32, name="sb_ps", tag="bank_w")
-        sa_ps = psum.tile([P, 2, P, 2], F32, name="sa_ps", tag="bank_s")
         for r in range(RUN):
             nc.tensor.transpose(
                 sb_ps[:, r, :], sb_raw[:, r : r + 1].to_broadcast([P, P]), ident[:]
@@ -124,12 +125,12 @@ def tile_attend_rollout_kernel(
             out=qg_sc[:].bitcast(I32).rearrange("p (t m) -> p t m", t=PACK),
             in_=qg_plain[:].bitcast(I32).rearrange("p (m t) -> p t m", t=PACK),
         )
-        place_scale_rows(nc.sync, qg_sc, qg_sc, ((1, 4), (3, 68)))
+        place_scale_rows(nc.sync, qg_sc, qg_sc, ((1, 4), (2, 8), (3, 12)))
         k2g_plain = big.tile([P, J], U8, name="k2g_plain", tag="keys_window", align_bytes=64)
         nc.vector.tensor_copy(k2g_plain[:], k2_sc[:].indirect(offs2_t[:]))
         k2g_sc = keep.tile([P, J], U8, name="k2g_sc", align_bytes=64)
         nc.vector.tensor_copy(out=k2g_sc[:].bitcast(I32), in_=k2g_plain[:].bitcast(I32))
-        place_spread_rows(nc, k2g_sc, k2g_sc, 1)
+        place_scale_rows(nc.sync, k2g_sc, k2g_sc, ((1, 4), (3, 68)))
         k_w = big.tile([P, T], U32, name="k_w", tag="keys_window", align_bytes=64)
         load_words(nc, k_w, keys_words)
         qg_w = keep.tile([P, I], U32, name="qg_w", align_bytes=64)
@@ -138,13 +139,16 @@ def tile_attend_rollout_kernel(
         )
         kg_first = keep.tile([P, HALF], U8, name="kg_first", align_bytes=64)
         nc.vector.tensor_copy(kg_first[:], k_sc[:].indirect(offs_t[:, 0 : HALF // 16]))
-        place_spread_rows(nc, kg_sc[:, 0:HALF], kg_first, 0)
+        nc.vector.tensor_copy(out=kg_sc[0][:].bitcast(I32), in_=kg_first[:].bitcast(I32))
+        place_spread_rows(nc, kg_sc[0], kg_sc[0], 1)
         k2g_w = gather_halves(nc, keep, k2_w, offs2_t, "k2g_w")
         kg_second = big.tile([P, HALF], U8, name="kg_second", tag="keys2_window", align_bytes=64)
         nc.vector.tensor_copy(kg_second[:], k_sc[:].indirect(offs_t[:, HALF // 16 : I // 16]))
-        place_spread_rows(nc, kg_sc[:, HALF:I], kg_second, 0)
+        place_spread_rows(nc, kg_sc[1], kg_second, 0)
+        sa_raw = keep.tile([P, RUN], F32, name="sa_raw", tag="k_sc", align_bytes=64)
+        nc.sync.dma_start(out=sa_raw[:], in_=sa.rearrange("o (p r) -> p (o r)", r=RUN))
 
-        b_ps = [psum.tile([P, J], F32, name="b_ps%d" % t) for t in range(PACK)]
+        b_ps = [psum.tile([P, J], F32, name="b_ps%d" % t, tag="bank_b%d" % t) for t in range(PACK)]
         for t in range(PACK):
             for h in range(2):
                 nc.tensor.matmul_mx(
@@ -168,12 +172,6 @@ def tile_attend_rollout_kernel(
                 out=r_exp[t][:], in_=b_ps[t][:], func=ACT.Exp, bias=negmax, scale=1.0, accum_out=b_sum[:, t : t + 1]
             )
 
-        sa_raw = keep.tile([P, RUN], F32, name="sa_raw", tag="slot_weights")
-        nc.sync.dma_start(out=sa_raw[:], in_=sa.rearrange("o (p r) -> p (o r)", r=RUN))
-        for r in range(RUN):
-            nc.tensor.transpose(
-                sa_ps[:].rearrange("q u (m r) e -> q r m u e", r=RUN)[:, r], sa_raw[:, r : r + 1].to_broadcast([P, P]), ident[:]
-            )
         early_negmax = keep.tile([P, 2], F32, name="early_negmax")
         for t in range(2):
             second_softmax(t, early_negmax[:, t : t + 1])
@@ -182,7 +180,12 @@ def tile_attend_rollout_kernel(
         for h in range(2):
             nc.tensor.matmul_mx(
                 out=a_ps[:, h * HALF : (h + 1) * HALF], lhsT=q_codes[:].bitcast(FP8X4), lhsT_scale=q_sc[:],
-                rhs=kg_w[h][:].bitcast(FP8X4), rhs_scale=kg_sc[:, h * HALF : (h + 1) * HALF], start=True, stop=True,
+                rhs=kg_w[h][:].bitcast(FP8X4), rhs_scale=kg_sc[h][:], start=True, stop=True,
+            )
+        sa_ps = psum.tile([P, 2, P, 2], F32, name="sa_ps", tag="bank_s")
+        for r in range(RUN):
+            nc.tensor.transpose(
+                sa_ps[:].rearrange("q u (m r) e -> q r m u e", r=RUN)[:, r], sa_raw[:, r : r + 1].to_broadcast([P, P]), ident[:]
             )
         a_negmax = keep.tile([P, 1], F32, name="a_negmax")
         a_sum = keep.tile([P, 1], F32, name="a_sum")
@@ -196,14 +199,13 @@ def tile_attend_rollout_kernel(
         )
         third_negmax = big.tile([P, 1], F32, name="third_negmax", tag="keys_window", align_bytes=64)
         second_softmax(2, third_negmax[:])
-        late_stats = keep.tile([P, 1 + PACK], F32, name="late_stats", tag="kg_w1", align_bytes=64)
+        late_stats = keep.tile([P, 1 + PACK], F32, name="late_stats", tag="k_sc", align_bytes=64)
         b_inv = late_stats[:, 1 : 1 + PACK]
         second_softmax(3, late_stats[:, 0:1])
         first_inv = keep.tile([P, 1], F32, name="first_inv")
         nc.vector.reciprocal(out=a_inv[:], in_=a_sum[:])
         nc.gpsimd.tensor_tensor(out=first_inv[:], in0=b_sum[:, 0:1], in1=minus_one[:], op=ALU.pow)
         nc.vector.reciprocal(out=b_inv[:, 1:3], in_=b_sum[:, 1:3])
-        nc.vector.reciprocal(out=b_inv[:, 3:4], in_=b_sum[:, 3:4])
         wt_ps = psum.tile([P, 2, Q], F32, name="wt_ps", tag="bank_w")
         for u in range(2):
             w_pair = keep.tile([P, P, 2], BF16, name="w_pair%d" % u, align_bytes=64)
@@ -212,6 +214,8 @@ def tile_attend_rollout_kernel(
                 in1=sa_ps[:, u, :, :], op0=ALU.mult, op1=ALU.mult,
             )
             nc.tensor.transpose(wt_ps[:, u, :], w_pair[:].rearrange("q p e -> q (p e)").bitcast(F32), ident[:])
+            if u == 0:
+                nc.vector.reciprocal(out=b_inv[:, 3:4], in_=b_sum[:, 3:4])
         wt_grp = keep.tile([P, Q, PACK], BF16, name="wt_grp", align_bytes=64)
         nc.scalar.copy(
             out=wt_grp[:].rearrange("p q t -> p (q t)").bitcast(F32).rearrange("p (q u) -> p q u", u=2),
@@ -231,10 +235,11 @@ def tile_attend_rollout_kernel(
             nc.scalar.activation(
                 out=pairs[:, :, 0, :, t], in_=r_exp[t][:].rearrange("p (h j) -> p h j", h=2), func=ACT.Copy, scale=factor[:]
             )
-        nc.vector.tensor_scalar(
-            out=pairs[:, :, 1, :, 0], in0=r_exp[2][:].rearrange("p (h j) -> p h j", h=2),
-            scalar1=b_inv[:, 2:3], scalar2=sb_col[:, 2:3], op0=ALU.mult, op1=ALU.mult,
-        )
+        for h in range(2):
+            nc.vector.tensor_scalar(
+                out=pairs[:, h, 1, :, 0], in0=r_exp[2][:, h * HALF : (h + 1) * HALF],
+                scalar1=b_inv[:, 2:3], scalar2=sb_col[:, 2:3], op0=ALU.mult, op1=ALU.mult,
+            )
         for h in range(2):
             nc.vector.tensor_scalar(
                 out=pairs[:, h, 1, :, 1], in0=r_exp[3][:, h * HALF : (h + 1) * HALF],
@@ -246,18 +251,17 @@ def tile_attend_rollout_kernel(
             x_codes.append(keep.tile([P, HALF], U32, name="x_codes%d" % h, align_bytes=64))
             x_sc.append(keep.tile([P, HALF], U8, name="x_sc%d" % h, align_bytes=64))
         for h in range(2):
-            nc.vector.tensor_copy(
+            (nc.vector.tensor_copy, nc.scalar.copy)[h](
                 out=x_grp[h][:].rearrange("p j t -> p (j t)").bitcast(F32).rearrange("p (j u) -> p j u", u=2),
                 in_=pairs[:, h].rearrange("p u j e -> p (u j e)").bitcast(F32).rearrange("p (u j) -> p j u", u=2),
             )
+        nc.vector.quantize_mx(
+            out=wt_codes[:].bitcast(FP8X4), scales=wt_sc[:], in_=wt_grp[:].rearrange("p q t -> p (q t)")
+        )
         for h in range(2):
             nc.vector.quantize_mx(
                 out=x_codes[h][:].bitcast(FP8X4), scales=x_sc[h][:], in_=x_grp[h][:].rearrange("p j t -> p (j t)")
             )
-            if h == 0:
-                nc.vector.quantize_mx(
-                    out=wt_codes[:].bitcast(FP8X4), scales=wt_sc[:], in_=wt_grp[:].rearrange("p q t -> p (q t)")
-                )
         for h in range(2):
             y_ps = psum.tile([P, HALF], F32, name="y_ps%d" % h, tag=("bank_a", "bank_c")[h])
             nc.tensor.matmul_mx(

@@ -79,13 +79,12 @@ def tile_attend_rollout_kernel(
         qp_w = big.tile([P, T], U32, name="qp_w")
         k2_w = big.tile([P, T], U32, name="k2_w", tag="keys2_window", align_bytes=64)
 
-        nc.vector.memset(k2_sc[:, 0 : T // 2].bitcast(I32), 0)
-        nc.gpsimd.memset(k2_sc[:, T // 2 : T].bitcast(I32), 0)
-        nc.vector.memset(qp_sc[64:P, :].bitcast(I32), 0)
-        nc.gpsimd.memset(qp_sc[32:64, :].bitcast(I32), 0)
+        nc.gpsimd.memset(k2_sc[:].bitcast(I32), 0)
         nc.vector.memset(k_sc[:].bitcast(I32), 0)
-        kg_sc = [keep.tile([P, HALF], U8, name="kg_sc%d" % h, align_bytes=64) for h in range(2)]
-        nc.vector.memset(kg_sc[1][:].bitcast(I32), 0)
+        nc.vector.memset(qp_sc[64:P, :].bitcast(I32), 0)
+        nc.vector.memset(qp_sc[32:64, :].bitcast(I32), 0)
+        kg_sc = keep.tile([P, I], U8, name="kg_sc", align_bytes=64)
+        nc.vector.memset(kg_sc[:].bitcast(I32), 0)
         make_identity(nc, ident[:])
         minus_one = keep.tile([P, 1], F32, name="minus_one")
         nc.gpsimd.memset(minus_one[:], -1.0)
@@ -94,11 +93,11 @@ def tile_attend_rollout_kernel(
         load_scales(nc, qp_sc, qpool_scales, 0, SCALE_ROWS, 0)
         load_scales(nc, qp_sc, qpool_scales, 0, SCALE_ROWS, SCALE_ROWS)
         nc.sync.dma_start(offs2_t[:], offs2)
-        nc.sync.dma_start(out=sb_raw[:], in_=sb.rearrange("(p r) o -> p (r o)", r=RUN))
         load_scales(nc, k2_sc, keys2_scales, 0, 8, 0)
         load_scales(nc, k2_sc, keys2_scales, 8, 8, 64)
-        load_words(nc, qp_w, qpool_words)
         load_spread_scales(nc, k_sc, keys_scales)
+        load_words(nc, qp_w, qpool_words)
+        nc.sync.dma_start(out=sb_raw[:], in_=sb.rearrange("(p r) o -> p (r o)", r=RUN))
         load_words(nc, k2_w, keys2_words)
         nc.sync.dma_start(out=q_raw[:], in_=query.rearrange("(p j) w -> p j w", j=PACK))
 
@@ -120,33 +119,27 @@ def tile_attend_rollout_kernel(
 
         qg_plain = keep.tile([P, I], U8, name="qg_plain", align_bytes=64)
         nc.vector.tensor_copy(qg_plain[:], qp_sc[:].indirect(offs_t[:]))
-        qg_sc = keep.tile([P, I], U8, name="qg_sc", align_bytes=64)
+        k2g_plain = big.tile([P, J], U8, name="k2g_plain", tag="keys_window", align_bytes=64)
+        nc.vector.tensor_copy(k2g_plain[:], k2_sc[:].indirect(offs2_t[:]))
+        qg_sc = keep.tile([P, I], U8, name="qg_sc", tag="k2_sc", align_bytes=64)
         nc.vector.tensor_copy(
             out=qg_sc[:].bitcast(I32).rearrange("p (t m) -> p t m", t=PACK),
             in_=qg_plain[:].bitcast(I32).rearrange("p (m t) -> p t m", t=PACK),
         )
         place_scale_rows(nc.sync, qg_sc, qg_sc, ((1, 4), (2, 8), (3, 12)))
-        k2g_plain = big.tile([P, J], U8, name="k2g_plain", tag="keys_window", align_bytes=64)
-        nc.vector.tensor_copy(k2g_plain[:], k2_sc[:].indirect(offs2_t[:]))
         k2g_sc = keep.tile([P, J], U8, name="k2g_sc", align_bytes=64)
         nc.vector.tensor_copy(out=k2g_sc[:].bitcast(I32), in_=k2g_plain[:].bitcast(I32))
         place_scale_rows(nc.sync, k2g_sc, k2g_sc, ((1, 4), (3, 68)))
         k_w = big.tile([P, T], U32, name="k_w", tag="keys_window", align_bytes=64)
         load_words(nc, k_w, keys_words)
+        kg_plain = keep.tile([P, I], U8, name="kg_plain", align_bytes=64)
+        nc.vector.tensor_copy(kg_plain[:], k_sc[:].indirect(offs_t[:]))
+        place_spread_rows(nc, kg_sc, kg_plain, 0)
         qg_w = keep.tile([P, I], U32, name="qg_w", align_bytes=64)
         nc.vector.tensor_copy(
             qg_w[:].rearrange("p (t m r) -> p m t r", t=PACK, r=RUN), qp_w[:].indirect(offs_t[:])
         )
-        kg_first = keep.tile([P, HALF], U8, name="kg_first", align_bytes=64)
-        nc.vector.tensor_copy(kg_first[:], k_sc[:].indirect(offs_t[:, 0 : HALF // 16]))
-        nc.vector.tensor_copy(out=kg_sc[0][:].bitcast(I32), in_=kg_first[:].bitcast(I32))
-        place_spread_rows(nc, kg_sc[0], kg_sc[0], 1)
         k2g_w = gather_halves(nc, keep, k2_w, offs2_t, "k2g_w")
-        kg_second = big.tile([P, HALF], U8, name="kg_second", tag="keys2_window", align_bytes=64)
-        nc.vector.tensor_copy(kg_second[:], k_sc[:].indirect(offs_t[:, HALF // 16 : I // 16]))
-        place_spread_rows(nc, kg_sc[1], kg_second, 0)
-        sa_raw = keep.tile([P, RUN], F32, name="sa_raw", tag="k_sc", align_bytes=64)
-        nc.sync.dma_start(out=sa_raw[:], in_=sa.rearrange("o (p r) -> p (o r)", r=RUN))
 
         b_ps = [psum.tile([P, J], F32, name="b_ps%d" % t, tag="bank_b%d" % t) for t in range(PACK)]
         for t in range(PACK):
@@ -162,6 +155,8 @@ def tile_attend_rollout_kernel(
         q_codes = keep.tile([P, Q], U32, name="q_codes", align_bytes=64)
         q_sc = keep.tile([P, Q], U8, name="q_sc", align_bytes=64)
         nc.vector.quantize_mx(out=q_codes[:].bitcast(FP8X4), scales=q_sc[:], in_=q_grp[:].rearrange("p w j -> p (w j)"))
+        sa_raw = keep.tile([P, RUN], F32, name="sa_raw", tag="q_grp", align_bytes=64)
+        nc.sync.dma_start(out=sa_raw[:], in_=sa.rearrange("o (p r) -> p (o r)", r=RUN))
         kg_w = gather_halves(nc, keep, k_w, offs_t, "kg_w")
         r_exp = [keep.tile([P, J], F32, name="r_exp%d" % t) for t in range(PACK)]
         b_sum = keep.tile([P, PACK], F32, name="b_sum")
@@ -180,7 +175,7 @@ def tile_attend_rollout_kernel(
         for h in range(2):
             nc.tensor.matmul_mx(
                 out=a_ps[:, h * HALF : (h + 1) * HALF], lhsT=q_codes[:].bitcast(FP8X4), lhsT_scale=q_sc[:],
-                rhs=kg_w[h][:].bitcast(FP8X4), rhs_scale=kg_sc[h][:], start=True, stop=True,
+                rhs=kg_w[h][:].bitcast(FP8X4), rhs_scale=kg_sc[:, h * HALF : (h + 1) * HALF], start=True, stop=True,
             )
         sa_ps = psum.tile([P, 2, P, 2], F32, name="sa_ps", tag="bank_s")
         for r in range(RUN):
@@ -199,7 +194,7 @@ def tile_attend_rollout_kernel(
         )
         third_negmax = big.tile([P, 1], F32, name="third_negmax", tag="keys_window", align_bytes=64)
         second_softmax(2, third_negmax[:])
-        late_stats = keep.tile([P, 1 + PACK], F32, name="late_stats", tag="k_sc", align_bytes=64)
+        late_stats = keep.tile([P, 1 + PACK], F32, name="late_stats", tag="q_grp", align_bytes=64)
         b_inv = late_stats[:, 1 : 1 + PACK]
         second_softmax(3, late_stats[:, 0:1])
         first_inv = keep.tile([P, 1], F32, name="first_inv")

@@ -15,45 +15,43 @@ ACT = mybir.ActivationFunctionType
 AXIS_X = mybir.AxisListType.X
 
 P = 128
+QUAD = 32
 PACK = 4
+RUN = 4
 D, T, I, J, Q = 512, 2048, 512, 512, 128
 HALF = J // 2
-RUN = 4
-FLOPS = 2 * D * Q * I + 2 * D * I * J + 2 * I * Q * J
-
+LIST_ROWS = 16
 SCALE_ROWS = 16
-ROW_STEP = 8
+QUAD_ROWS = 4
+ROW_STEP = P // SCALE_ROWS
+OUT_FACTOR = 512.0
+FLOPS = 2 * D * Q * I + 2 * D * I * J + 2 * I * Q * J
 
 
 def load_words(nc, tile, words):
     nc.sync.dma_start(out=tile[:].bitcast(I32), in_=words[0].rearrange("p n t -> p (n t)").bitcast(I32))
 
 
-def load_scales(nc, tile, scales, first_row=0, rows=SCALE_ROWS, partition=0):
+def load_scale_rows(nc, tile, scales, first_row, rows, partition):
     nc.sync.dma_start(
         out=tile[partition : partition + rows, :].bitcast(I32), in_=scales[0].bitcast(I32)[first_row : first_row + rows, :]
     )
 
 
-def load_spread_scales(nc, tile, scales):
-    nc.sync.dma_start(out=tile[0:P:ROW_STEP, :].bitcast(I32), in_=scales[0].bitcast(I32))
-
-
-def place_spread_rows(nc, plane, source, first):
-    for r in range(first, 4):
-        nc.sync.dma_start(out=plane[r:P:32, :].bitcast(I32), in_=source[ROW_STEP * r : P : 32, :].bitcast(I32))
-
-
-def place_scale_rows(queue, plane, source, moves):
-    for quad, row in moves:
-        queue.dma_start(out=plane[32 * quad : 32 * quad + 4, :].bitcast(I32), in_=source[row : row + 4, :].bitcast(I32))
+def move_quadrant_rows(nc, plane, moves):
+    for quad, partition in moves:
+        nc.sync.dma_start(
+            out=plane[QUAD * quad : QUAD * quad + QUAD_ROWS, :].bitcast(I32),
+            in_=plane[partition : partition + QUAD_ROWS, :].bitcast(I32),
+        )
 
 
 def gather_halves(nc, pool, window, offsets, name):
+    columns = HALF // LIST_ROWS
     halves = []
     for h in range(2):
-        part = pool.tile([P, HALF], U32, name="%s%d" % (name, h), tag="%s%d" % (name, h), align_bytes=64)
-        nc.vector.tensor_copy(part[:], window[:].indirect(offsets[:, h * (HALF // 16) : (h + 1) * (HALF // 16)]))
+        part = pool.tile([P, HALF], U32, name="%s%d" % (name, h), align_bytes=64)
+        nc.vector.tensor_copy(part[:], window[:].indirect(offsets[:, h * columns : (h + 1) * columns]))
         halves.append(part)
     return halves
 
@@ -67,49 +65,44 @@ def tile_attend_rollout_kernel(
         big = ctx.enter_context(tc.tile_pool(name="big", bufs=1))
         psum = ctx.enter_context(tc.psum_pool(name="psum", bufs=1))
 
-        offs_t = keep.tile([P, I // 16], U16, name="offs_t")
-        offs2_t = keep.tile([P, J // 16], U16, name="offs2_t")
+        offs_t = keep.tile([P, I // LIST_ROWS], U16, name="offs_t")
+        offs2_t = keep.tile([P, J // LIST_ROWS], U16, name="offs2_t")
         k_sc = keep.tile([P, T], U8, name="k_sc", align_bytes=64)
         qp_sc = keep.tile([P, T], U8, name="qp_sc", align_bytes=64)
-        k2_sc = keep.tile([P, T], U8, name="k2_sc", align_bytes=64)
+        k2_sc = keep.tile([P, T], U8, name="k2_sc", tag="keys2_scale_window", align_bytes=64)
         ident = keep.tile([P, P], F32, name="ident")
-        sb_raw = keep.tile([P, RUN], F32, name="sb_raw", tag="slot_weights")
-
+        sb_raw = keep.tile([P, RUN], F32, name="sb_raw")
         q_raw = keep.tile([P, PACK, Q], F32, name="q_raw")
         qp_w = big.tile([P, T], U32, name="qp_w")
-        k2_w = big.tile([P, T], U32, name="k2_w", tag="keys2_window", align_bytes=64)
+        k2_w = big.tile([P, T], U32, name="k2_w", align_bytes=64)
 
         nc.gpsimd.memset(k2_sc[:].bitcast(I32), 0)
         nc.vector.memset(k_sc[:].bitcast(I32), 0)
-        nc.vector.memset(qp_sc[64:P, :].bitcast(I32), 0)
-        nc.vector.memset(qp_sc[32:64, :].bitcast(I32), 0)
-        kg_sc = keep.tile([P, I], U8, name="kg_sc", align_bytes=64)
-        nc.vector.memset(kg_sc[:].bitcast(I32), 0)
+        nc.vector.memset(qp_sc[2 * QUAD : P, :].bitcast(I32), 0)
+        nc.vector.memset(qp_sc[QUAD : 2 * QUAD, :].bitcast(I32), 0)
         make_identity(nc, ident[:])
         minus_one = keep.tile([P, 1], F32, name="minus_one")
         nc.gpsimd.memset(minus_one[:], -1.0)
 
         nc.sync.dma_start(offs_t[:], offs)
-        load_scales(nc, qp_sc, qpool_scales, 0, SCALE_ROWS, 0)
-        load_scales(nc, qp_sc, qpool_scales, 0, SCALE_ROWS, SCALE_ROWS)
+        for partition in (0, SCALE_ROWS):
+            load_scale_rows(nc, qp_sc, qpool_scales, 0, SCALE_ROWS, partition)
         nc.sync.dma_start(offs2_t[:], offs2)
-        load_scales(nc, k2_sc, keys2_scales, 0, 8, 0)
-        load_scales(nc, k2_sc, keys2_scales, 8, 8, 64)
-        load_spread_scales(nc, k_sc, keys_scales)
+        for half in range(2):
+            load_scale_rows(nc, k2_sc, keys2_scales, half * SCALE_ROWS // 2, SCALE_ROWS // 2, half * 2 * QUAD)
+        nc.sync.dma_start(out=k_sc[0:P:ROW_STEP, :].bitcast(I32), in_=keys_scales[0].bitcast(I32))
         load_words(nc, qp_w, qpool_words)
         nc.sync.dma_start(out=sb_raw[:], in_=sb.rearrange("(p r) o -> p (r o)", r=RUN))
         load_words(nc, k2_w, keys2_words)
         nc.sync.dma_start(out=q_raw[:], in_=query.rearrange("(p j) w -> p j w", j=PACK))
 
-        sb_ps = psum.tile([P, PACK, P], F32, name="sb_ps", tag="bank_w")
+        sb_ps = psum.tile([P, RUN, P], F32, name="sb_ps", tag="bank_w")
         for r in range(RUN):
-            nc.tensor.transpose(
-                sb_ps[:, r, :], sb_raw[:, r : r + 1].to_broadcast([P, P]), ident[:]
-            )
+            nc.tensor.transpose(sb_ps[:, r, :], sb_raw[:, r : r + 1].to_broadcast([P, P]), ident[:])
         sb_rows = keep.tile([P, PACK, P], F32, name="sb_rows")
         nc.scalar.activation(
             out=sb_rows[:].rearrange("q t (m r) -> q t m r", r=RUN),
-            in_=sb_ps[:].rearrange("q r (m t) -> q t m r", t=PACK), func=ACT.Copy, scale=512.0,
+            in_=sb_ps[:].rearrange("q r (m t) -> q t m r", t=PACK), func=ACT.Copy, scale=OUT_FACTOR,
         )
         cols_ps = psum.tile([P, PACK, P], F32, name="cols_ps", tag="bank_c")
         for t in range(PACK):
@@ -121,27 +114,27 @@ def tile_attend_rollout_kernel(
         nc.vector.tensor_copy(qg_plain[:], qp_sc[:].indirect(offs_t[:]))
         k2g_plain = big.tile([P, J], U8, name="k2g_plain", tag="keys_window", align_bytes=64)
         nc.vector.tensor_copy(k2g_plain[:], k2_sc[:].indirect(offs2_t[:]))
-        qg_sc = keep.tile([P, I], U8, name="qg_sc", tag="k2_sc", align_bytes=64)
+        qg_sc = keep.tile([P, I], U8, name="qg_sc", tag="keys2_scale_window", align_bytes=64)
         nc.vector.tensor_copy(
             out=qg_sc[:].bitcast(I32).rearrange("p (t m) -> p t m", t=PACK),
             in_=qg_plain[:].bitcast(I32).rearrange("p (m t) -> p t m", t=PACK),
         )
-        place_scale_rows(nc.sync, qg_sc, qg_sc, ((1, 4), (2, 8), (3, 12)))
+        move_quadrant_rows(nc, qg_sc, [(quad, QUAD_ROWS * quad) for quad in (1, 2, 3)])
         k2g_sc = keep.tile([P, J], U8, name="k2g_sc", align_bytes=64)
         nc.vector.tensor_copy(out=k2g_sc[:].bitcast(I32), in_=k2g_plain[:].bitcast(I32))
-        place_scale_rows(nc.sync, k2g_sc, k2g_sc, ((1, 4), (3, 68)))
+        move_quadrant_rows(nc, k2g_sc, [(quad, QUAD * (quad - 1) + QUAD_ROWS) for quad in (1, 3)])
         k_w = big.tile([P, T], U32, name="k_w", tag="keys_window", align_bytes=64)
         load_words(nc, k_w, keys_words)
         kg_plain = keep.tile([P, I], U8, name="kg_plain", align_bytes=64)
         nc.vector.tensor_copy(kg_plain[:], k_sc[:].indirect(offs_t[:]))
-        place_spread_rows(nc, kg_sc, kg_plain, 0)
-        qg_w = keep.tile([P, I], U32, name="qg_w", align_bytes=64)
-        nc.vector.tensor_copy(
-            qg_w[:].rearrange("p (t m r) -> p m t r", t=PACK, r=RUN), qp_w[:].indirect(offs_t[:])
-        )
-        k2g_w = gather_halves(nc, keep, k2_w, offs2_t, "k2g_w")
+        kg_sc = keep.tile([P, I], U8, name="kg_sc", align_bytes=64)
+        for r in range(QUAD_ROWS):
+            nc.sync.dma_start(out=kg_sc[r:P:QUAD, :].bitcast(I32), in_=kg_plain[ROW_STEP * r : P : QUAD, :].bitcast(I32))
 
-        b_ps = [psum.tile([P, J], F32, name="b_ps%d" % t, tag="bank_b%d" % t) for t in range(PACK)]
+        qg_w = keep.tile([P, I], U32, name="qg_w", align_bytes=64)
+        nc.vector.tensor_copy(qg_w[:].rearrange("p (t m r) -> p m t r", t=PACK, r=RUN), qp_w[:].indirect(offs_t[:]))
+        k2g_w = gather_halves(nc, keep, k2_w, offs2_t, "k2g_w")
+        b_ps = [psum.tile([P, J], F32, name="b_ps%d" % t) for t in range(PACK)]
         for t in range(PACK):
             for h in range(2):
                 nc.tensor.matmul_mx(
@@ -150,14 +143,16 @@ def tile_attend_rollout_kernel(
                     rhs=k2g_w[h][:].bitcast(FP8X4), rhs_scale=k2g_sc[:, h * HALF : (h + 1) * HALF],
                     start=True, stop=True,
                 )
-        q_grp = keep.tile([P, Q, PACK], BF16, name="q_grp", align_bytes=64)
+
+        q_grp = keep.tile([P, Q, PACK], BF16, name="q_grp", tag="query_buffer", align_bytes=64)
         nc.scalar.copy(out=q_grp[:], in_=q_raw[:].rearrange("p j w -> p w j"))
         q_codes = keep.tile([P, Q], U32, name="q_codes", align_bytes=64)
         q_sc = keep.tile([P, Q], U8, name="q_sc", align_bytes=64)
         nc.vector.quantize_mx(out=q_codes[:].bitcast(FP8X4), scales=q_sc[:], in_=q_grp[:].rearrange("p w j -> p (w j)"))
-        sa_raw = keep.tile([P, RUN], F32, name="sa_raw", tag="q_grp", align_bytes=64)
+        sa_raw = keep.tile([P, RUN], F32, name="sa_raw", tag="query_buffer", align_bytes=64)
         nc.sync.dma_start(out=sa_raw[:], in_=sa.rearrange("o (p r) -> p (o r)", r=RUN))
         kg_w = gather_halves(nc, keep, k_w, offs_t, "kg_w")
+
         r_exp = [keep.tile([P, J], F32, name="r_exp%d" % t) for t in range(PACK)]
         b_sum = keep.tile([P, PACK], F32, name="b_sum")
 
@@ -177,7 +172,7 @@ def tile_attend_rollout_kernel(
                 out=a_ps[:, h * HALF : (h + 1) * HALF], lhsT=q_codes[:].bitcast(FP8X4), lhsT_scale=q_sc[:],
                 rhs=kg_w[h][:].bitcast(FP8X4), rhs_scale=kg_sc[:, h * HALF : (h + 1) * HALF], start=True, stop=True,
             )
-        sa_ps = psum.tile([P, 2, P, 2], F32, name="sa_ps", tag="bank_s")
+        sa_ps = psum.tile([P, 2, P, 2], F32, name="sa_ps")
         for r in range(RUN):
             nc.tensor.transpose(
                 sa_ps[:].rearrange("q u (m r) e -> q r m u e", r=RUN)[:, r], sa_raw[:, r : r + 1].to_broadcast([P, P]), ident[:]
@@ -192,25 +187,29 @@ def tile_attend_rollout_kernel(
             in_=a_ps[:].rearrange("q (m t r) -> q t m r", t=PACK, r=RUN),
             func=ACT.Exp, bias=a_negmax[:], scale=1.0, accum_out=a_sum[:],
         )
+
         third_negmax = big.tile([P, 1], F32, name="third_negmax", tag="keys_window", align_bytes=64)
         second_softmax(2, third_negmax[:])
-        late_stats = keep.tile([P, 1 + PACK], F32, name="late_stats", tag="q_grp", align_bytes=64)
-        b_inv = late_stats[:, 1 : 1 + PACK]
+        late_stats = keep.tile([P, PACK], F32, name="late_stats", tag="query_buffer", align_bytes=64)
         second_softmax(3, late_stats[:, 0:1])
-        first_inv = keep.tile([P, 1], F32, name="first_inv")
         nc.vector.reciprocal(out=a_inv[:], in_=a_sum[:])
+        first_inv = keep.tile([P, 1], F32, name="first_inv")
         nc.gpsimd.tensor_tensor(out=first_inv[:], in0=b_sum[:, 0:1], in1=minus_one[:], op=ALU.pow)
-        nc.vector.reciprocal(out=b_inv[:, 1:3], in_=b_sum[:, 1:3])
+        nc.vector.reciprocal(out=late_stats[:, 1:3], in_=b_sum[:, 1:3])
+
         wt_ps = psum.tile([P, 2, Q], F32, name="wt_ps", tag="bank_w")
-        for u in range(2):
+
+        def weigh_and_turn(u):
             w_pair = keep.tile([P, P, 2], BF16, name="w_pair%d" % u, align_bytes=64)
             nc.vector.scalar_tensor_tensor(
                 out=w_pair[:], in0=p_exp[:, 2 * u : 2 * u + 2, :].rearrange("q e p -> q p e"), scalar=a_inv[:],
                 in1=sa_ps[:, u, :, :], op0=ALU.mult, op1=ALU.mult,
             )
             nc.tensor.transpose(wt_ps[:, u, :], w_pair[:].rearrange("q p e -> q (p e)").bitcast(F32), ident[:])
-            if u == 0:
-                nc.vector.reciprocal(out=b_inv[:, 3:4], in_=b_sum[:, 3:4])
+
+        weigh_and_turn(0)
+        nc.vector.reciprocal(out=late_stats[:, 3:4], in_=b_sum[:, 3:4])
+        weigh_and_turn(1)
         wt_grp = keep.tile([P, Q, PACK], BF16, name="wt_grp", align_bytes=64)
         nc.scalar.copy(
             out=wt_grp[:].rearrange("p q t -> p (q t)").bitcast(F32).rearrange("p (q u) -> p q u", u=2),
@@ -220,52 +219,47 @@ def tile_attend_rollout_kernel(
         wt_sc = keep.tile([P, Q], U8, name="wt_sc", align_bytes=64)
 
         pairs = keep.tile([P, 2, 2, HALF, 2], BF16, name="pairs", align_bytes=64)
-        for t in range(2):
-            inv = first_inv[:] if t == 0 else b_inv[:, t : t + 1]
-            factor = keep.tile([P, 1], F32, name="factor%d" % t)
-            if t == 0:
-                nc.scalar.activation(out=factor[:], in_=inv, func=ACT.Copy, scale=sb_col[:, t : t + 1])
-            else:
-                nc.gpsimd.tensor_tensor(out=factor[:], in0=inv, in1=sb_col[:, t : t + 1], op=ALU.mult)
+
+        def scale_on_scalar(t, factor):
             nc.scalar.activation(
                 out=pairs[:, :, 0, :, t], in_=r_exp[t][:].rearrange("p (h j) -> p h j", h=2), func=ACT.Copy, scale=factor[:]
             )
-        for h in range(2):
-            nc.vector.tensor_scalar(
-                out=pairs[:, h, 1, :, 0], in0=r_exp[2][:, h * HALF : (h + 1) * HALF],
-                scalar1=b_inv[:, 2:3], scalar2=sb_col[:, 2:3], op0=ALU.mult, op1=ALU.mult,
-            )
-        for h in range(2):
-            nc.vector.tensor_scalar(
-                out=pairs[:, h, 1, :, 1], in0=r_exp[3][:, h * HALF : (h + 1) * HALF],
-                scalar1=b_inv[:, 3:4], scalar2=sb_col[:, 3:4], op0=ALU.mult, op1=ALU.mult,
-            )
+
+        first_factor = keep.tile([P, 1], F32, name="first_factor")
+        nc.scalar.activation(out=first_factor[:], in_=first_inv[:], func=ACT.Copy, scale=sb_col[:, 0:1])
+        scale_on_scalar(0, first_factor)
+        second_factor = keep.tile([P, 1], F32, name="second_factor")
+        nc.gpsimd.tensor_tensor(out=second_factor[:], in0=late_stats[:, 1:2], in1=sb_col[:, 1:2], op=ALU.mult)
+        scale_on_scalar(1, second_factor)
+        for t in (2, 3):
+            for h in range(2):
+                nc.vector.tensor_scalar(
+                    out=pairs[:, h, 1, :, t - 2], in0=r_exp[t][:, h * HALF : (h + 1) * HALF],
+                    scalar1=late_stats[:, t : t + 1], scalar2=sb_col[:, t : t + 1], op0=ALU.mult, op1=ALU.mult,
+                )
+
         x_grp, x_codes, x_sc = [], [], []
         for h in range(2):
             x_grp.append(keep.tile([P, HALF, PACK], BF16, name="x_grp%d" % h, align_bytes=64))
             x_codes.append(keep.tile([P, HALF], U32, name="x_codes%d" % h, align_bytes=64))
             x_sc.append(keep.tile([P, HALF], U8, name="x_sc%d" % h, align_bytes=64))
-        for h in range(2):
-            (nc.vector.tensor_copy, nc.scalar.copy)[h](
+        for h, copy in enumerate((nc.vector.tensor_copy, nc.scalar.copy)):
+            copy(
                 out=x_grp[h][:].rearrange("p j t -> p (j t)").bitcast(F32).rearrange("p (j u) -> p j u", u=2),
                 in_=pairs[:, h].rearrange("p u j e -> p (u j e)").bitcast(F32).rearrange("p (u j) -> p j u", u=2),
             )
-        nc.vector.quantize_mx(
-            out=wt_codes[:].bitcast(FP8X4), scales=wt_sc[:], in_=wt_grp[:].rearrange("p q t -> p (q t)")
-        )
+        nc.vector.quantize_mx(out=wt_codes[:].bitcast(FP8X4), scales=wt_sc[:], in_=wt_grp[:].rearrange("p q t -> p (q t)"))
         for h in range(2):
             nc.vector.quantize_mx(
                 out=x_codes[h][:].bitcast(FP8X4), scales=x_sc[h][:], in_=x_grp[h][:].rearrange("p j t -> p (j t)")
             )
-        for h in range(2):
-            y_ps = psum.tile([P, HALF], F32, name="y_ps%d" % h, tag=("bank_a", "bank_c")[h])
+
+        for h, (bank, copy) in enumerate((("bank_a", nc.scalar.copy), ("bank_c", nc.vector.tensor_copy))):
+            y_ps = psum.tile([P, HALF], F32, name="y_ps%d" % h, tag=bank)
             nc.tensor.matmul_mx(
                 out=y_ps[:], lhsT=wt_codes[:].bitcast(FP8X4), lhsT_scale=wt_sc[:],
                 rhs=x_codes[h][:].bitcast(FP8X4), rhs_scale=x_sc[h][:], start=True, stop=True,
             )
             y_sb = keep.tile([P, HALF], F32, name="y_sb%d" % h)
-            if h == 0:
-                nc.scalar.copy(out=y_sb[:], in_=y_ps[:])
-            else:
-                nc.vector.tensor_copy(out=y_sb[:], in_=y_ps[:])
+            copy(out=y_sb[:], in_=y_ps[:])
             nc.sync.dma_start(out=out[:, h * HALF : (h + 1) * HALF], in_=y_sb[:])

@@ -32,8 +32,8 @@ def load_words(nc, tile, words):
     nc.sync.dma_start(out=tile[:].bitcast(I32), in_=words[0].rearrange("p n t -> p (n t)").bitcast(I32))
 
 
-def load_scale_rows(nc, tile, scales, first_row, rows, partition):
-    nc.sync.dma_start(
+def load_scale_rows(queue, tile, scales, first_row, rows, partition):
+    queue.dma_start(
         out=tile[partition : partition + rows, :].bitcast(I32), in_=scales[0].bitcast(I32)[first_row : first_row + rows, :]
     )
 
@@ -85,11 +85,11 @@ def tile_attend_rollout_kernel(
         nc.gpsimd.memset(minus_one[:], -1.0)
 
         nc.sync.dma_start(offs_t[:], offs)
-        for partition in (0, SCALE_ROWS):
-            load_scale_rows(nc, qp_sc, qpool_scales, 0, SCALE_ROWS, partition)
+        for queue, partition in ((nc.scalar, 0), (nc.sync, SCALE_ROWS)):
+            load_scale_rows(queue, qp_sc, qpool_scales, 0, SCALE_ROWS, partition)
         nc.sync.dma_start(offs2_t[:], offs2)
         for half in range(2):
-            load_scale_rows(nc, k2_sc, keys2_scales, half * SCALE_ROWS // 2, SCALE_ROWS // 2, half * 2 * QUAD)
+            load_scale_rows(nc.sync, k2_sc, keys2_scales, half * SCALE_ROWS // 2, SCALE_ROWS // 2, half * 2 * QUAD)
         nc.sync.dma_start(out=k_sc[0:P:ROW_STEP, :].bitcast(I32), in_=keys_scales[0].bitcast(I32))
         load_words(nc, qp_w, qpool_words)
         nc.sync.dma_start(out=sb_raw[:], in_=sb.rearrange("(p r) o -> p (r o)", r=RUN))
@@ -135,7 +135,7 @@ def tile_attend_rollout_kernel(
         nc.vector.tensor_copy(qg_w[:].rearrange("p (t m r) -> p m t r", t=PACK, r=RUN), qp_w[:].indirect(offs_t[:]))
         k2g_w = gather_halves(nc, keep, k2_w, offs2_t, "k2g_w")
         b_ps = [psum.tile([P, J], F32, name="b_ps%d" % t) for t in range(PACK)]
-        for t in range(PACK):
+        for t in (0, 2, 3, 1):
             for h in range(2):
                 nc.tensor.matmul_mx(
                     out=b_ps[t][:, h * HALF : (h + 1) * HALF],
@@ -155,6 +155,7 @@ def tile_attend_rollout_kernel(
 
         r_exp = [keep.tile([P, J], F32, name="r_exp%d" % t) for t in range(PACK)]
         b_sum = keep.tile([P, PACK], F32, name="b_sum")
+        pairs = [keep.tile([P, 2, HALF, 2], BF16, name="pairs%d" % h, align_bytes=64) for h in range(2)]
 
         def second_softmax(t, negmax):
             nc.vector.tensor_reduce(out=negmax, in_=b_ps[t][:], axis=AXIS_X, op=ALU.max, negate=True)
@@ -162,9 +163,34 @@ def tile_attend_rollout_kernel(
                 out=r_exp[t][:], in_=b_ps[t][:], func=ACT.Exp, bias=negmax, scale=1.0, accum_out=b_sum[:, t : t + 1]
             )
 
+        def scale_halves(engine, t, inv):
+            for h in range(2):
+                engine.tensor_scalar(
+                    out=pairs[h][:, t // 2, :, t % 2], in0=r_exp[t][:, h * HALF : (h + 1) * HALF],
+                    scalar1=inv, scalar2=sb_col[:, t : t + 1], op0=ALU.mult, op1=ALU.mult,
+                )
+
+        def invert_on_gpsimd(t):
+            inv = keep.tile([P, 1], F32, name="inv%d" % t)
+            nc.gpsimd.tensor_tensor(out=inv[:], in0=b_sum[:, t : t + 1], in1=minus_one[:], op=ALU.pow)
+            return inv
+
         early_negmax = keep.tile([P, 2], F32, name="early_negmax")
-        for t in range(2):
-            second_softmax(t, early_negmax[:, t : t + 1])
+        second_softmax(0, early_negmax[:, 0:1])
+        second_softmax(2, early_negmax[:, 1:2])
+        third_negmax = keep.tile([P, 1], F32, name="third_negmax", tag="late_negmax")
+        second_softmax(3, third_negmax[:])
+        inv0 = invert_on_gpsimd(0)
+        first_factor = keep.tile([P, 1], F32, name="first_factor")
+        nc.scalar.activation(out=first_factor[:], in_=inv0[:], func=ACT.Copy, scale=sb_col[:, 0:1])
+        for h in range(2):
+            nc.scalar.activation(
+                out=pairs[h][:, 0, :, 0], in_=r_exp[0][:, h * HALF : (h + 1) * HALF], func=ACT.Copy, scale=first_factor[:]
+            )
+        scale_halves(nc.gpsimd, 2, invert_on_gpsimd(2)[:])
+        scale_halves(nc.gpsimd, 3, invert_on_gpsimd(3)[:])
+        last_negmax = keep.tile([P, 1], F32, name="last_negmax", tag="late_negmax")
+        second_softmax(1, last_negmax[:])
 
         a_ps = psum.tile([P, I], F32, name="a_ps", tag="bank_a")
         for h in range(2):
@@ -188,14 +214,10 @@ def tile_attend_rollout_kernel(
             func=ACT.Exp, bias=a_negmax[:], scale=1.0, accum_out=a_sum[:],
         )
 
-        third_negmax = big.tile([P, 1], F32, name="third_negmax", tag="keys_window", align_bytes=64)
-        second_softmax(2, third_negmax[:])
-        late_stats = keep.tile([P, PACK], F32, name="late_stats", tag="query_buffer", align_bytes=64)
-        second_softmax(3, late_stats[:, 0:1])
+        inv1 = keep.tile([P, 1], F32, name="inv1", tag="query_buffer", align_bytes=64)
+        nc.vector.reciprocal(out=inv1[:], in_=b_sum[:, 1:2])
+        scale_halves(nc.vector, 1, inv1[:])
         nc.vector.reciprocal(out=a_inv[:], in_=a_sum[:])
-        first_inv = keep.tile([P, 1], F32, name="first_inv")
-        nc.gpsimd.tensor_tensor(out=first_inv[:], in0=b_sum[:, 0:1], in1=minus_one[:], op=ALU.pow)
-        nc.vector.reciprocal(out=late_stats[:, 1:3], in_=b_sum[:, 1:3])
 
         wt_ps = psum.tile([P, 2, Q], F32, name="wt_ps", tag="bank_w")
 
@@ -208,7 +230,6 @@ def tile_attend_rollout_kernel(
             nc.tensor.transpose(wt_ps[:, u, :], w_pair[:].rearrange("q p e -> q (p e)").bitcast(F32), ident[:])
 
         weigh_and_turn(0)
-        nc.vector.reciprocal(out=late_stats[:, 3:4], in_=b_sum[:, 3:4])
         weigh_and_turn(1)
         wt_grp = keep.tile([P, Q, PACK], BF16, name="wt_grp", align_bytes=64)
         nc.scalar.copy(
@@ -218,41 +239,21 @@ def tile_attend_rollout_kernel(
         wt_codes = keep.tile([P, Q], U32, name="wt_codes", align_bytes=64)
         wt_sc = keep.tile([P, Q], U8, name="wt_sc", align_bytes=64)
 
-        pairs = keep.tile([P, 2, 2, HALF, 2], BF16, name="pairs", align_bytes=64)
-
-        def scale_on_scalar(t, factor):
-            nc.scalar.activation(
-                out=pairs[:, :, 0, :, t], in_=r_exp[t][:].rearrange("p (h j) -> p h j", h=2), func=ACT.Copy, scale=factor[:]
-            )
-
-        first_factor = keep.tile([P, 1], F32, name="first_factor")
-        nc.scalar.activation(out=first_factor[:], in_=first_inv[:], func=ACT.Copy, scale=sb_col[:, 0:1])
-        scale_on_scalar(0, first_factor)
-        second_factor = keep.tile([P, 1], F32, name="second_factor")
-        nc.gpsimd.tensor_tensor(out=second_factor[:], in0=late_stats[:, 1:2], in1=sb_col[:, 1:2], op=ALU.mult)
-        scale_on_scalar(1, second_factor)
-        for t in (2, 3):
-            for h in range(2):
-                nc.vector.tensor_scalar(
-                    out=pairs[:, h, 1, :, t - 2], in0=r_exp[t][:, h * HALF : (h + 1) * HALF],
-                    scalar1=late_stats[:, t : t + 1], scalar2=sb_col[:, t : t + 1], op0=ALU.mult, op1=ALU.mult,
-                )
-
         x_grp, x_codes, x_sc = [], [], []
         for h in range(2):
             x_grp.append(keep.tile([P, HALF, PACK], BF16, name="x_grp%d" % h, align_bytes=64))
             x_codes.append(keep.tile([P, HALF], U32, name="x_codes%d" % h, align_bytes=64))
             x_sc.append(keep.tile([P, HALF], U8, name="x_sc%d" % h, align_bytes=64))
-        for h, copy in enumerate((nc.vector.tensor_copy, nc.scalar.copy)):
-            copy(
+        for h in range(2):
+            nc.scalar.copy(
                 out=x_grp[h][:].rearrange("p j t -> p (j t)").bitcast(F32).rearrange("p (j u) -> p j u", u=2),
-                in_=pairs[:, h].rearrange("p u j e -> p (u j e)").bitcast(F32).rearrange("p (u j) -> p j u", u=2),
+                in_=pairs[h][:].rearrange("p u j e -> p (u j e)").bitcast(F32).rearrange("p (u j) -> p j u", u=2),
             )
-        nc.vector.quantize_mx(out=wt_codes[:].bitcast(FP8X4), scales=wt_sc[:], in_=wt_grp[:].rearrange("p q t -> p (q t)"))
         for h in range(2):
             nc.vector.quantize_mx(
                 out=x_codes[h][:].bitcast(FP8X4), scales=x_sc[h][:], in_=x_grp[h][:].rearrange("p j t -> p (j t)")
             )
+        nc.vector.quantize_mx(out=wt_codes[:].bitcast(FP8X4), scales=wt_sc[:], in_=wt_grp[:].rearrange("p q t -> p (q t)"))
 
         for h, (bank, copy) in enumerate((("bank_a", nc.scalar.copy), ("bank_c", nc.vector.tensor_copy))):
             y_ps = psum.tile([P, HALF], F32, name="y_ps%d" % h, tag=bank)

@@ -81,11 +81,11 @@ def tile_attend_rollout_kernel(
         nc.vector.memset(qp_sc[2 * QUAD : P, :].bitcast(I32), 0)
         nc.vector.memset(qp_sc[QUAD : 2 * QUAD, :].bitcast(I32), 0)
         make_identity(nc, ident[:])
-        minus_one = keep.tile([P, 1], F32, name="minus_one")
+        minus_one = keep.tile([P, 2], F32, name="minus_one")
         nc.gpsimd.memset(minus_one[:], -1.0)
 
         nc.sync.dma_start(offs_t[:], offs)
-        for queue, partition in ((nc.scalar, 0), (nc.sync, SCALE_ROWS)):
+        for queue, partition in ((nc.sync, 0), (nc.sync, SCALE_ROWS)):
             load_scale_rows(queue, qp_sc, qpool_scales, 0, SCALE_ROWS, partition)
         nc.sync.dma_start(offs2_t[:], offs2)
         for half in range(2):
@@ -163,32 +163,33 @@ def tile_attend_rollout_kernel(
                 out=r_exp[t][:], in_=b_ps[t][:], func=ACT.Exp, bias=negmax, scale=1.0, accum_out=b_sum[:, t : t + 1]
             )
 
-        def scale_halves(engine, t, inv):
-            for h in range(2):
-                engine.tensor_scalar(
-                    out=pairs[h][:, t // 2, :, t % 2], in0=r_exp[t][:, h * HALF : (h + 1) * HALF],
-                    scalar1=inv, scalar2=sb_col[:, t : t + 1], op0=ALU.mult, op1=ALU.mult,
-                )
+        def scale_on_gpsimd(t, h, inv):
+            nc.gpsimd.tensor_scalar(
+                out=pairs[h][:, t // 2, :, t % 2], in0=r_exp[t][:, h * HALF : (h + 1) * HALF],
+                scalar1=inv, scalar2=sb_col[:, t : t + 1], op0=ALU.mult, op1=ALU.mult,
+            )
 
-        def invert_on_gpsimd(t):
-            inv = keep.tile([P, 1], F32, name="inv%d" % t)
-            nc.gpsimd.tensor_tensor(out=inv[:], in0=b_sum[:, t : t + 1], in1=minus_one[:], op=ALU.pow)
-            return inv
+        def scale_on_scalar(t, factor):
+            for h in (1, 0):
+                nc.scalar.activation(
+                    out=pairs[h][:, t // 2, :, t % 2], in_=r_exp[t][:, h * HALF : (h + 1) * HALF], func=ACT.Copy, scale=factor[:]
+                )
 
         early_negmax = keep.tile([P, 2], F32, name="early_negmax")
         second_softmax(0, early_negmax[:, 0:1])
         second_softmax(2, early_negmax[:, 1:2])
         third_negmax = keep.tile([P, 1], F32, name="third_negmax", tag="late_negmax")
         second_softmax(3, third_negmax[:])
-        inv0 = invert_on_gpsimd(0)
+        inv0 = keep.tile([P, 1], F32, name="inv0")
+        nc.gpsimd.tensor_tensor(out=inv0[:], in0=b_sum[:, 0:1], in1=minus_one[:, 0:1], op=ALU.pow)
         first_factor = keep.tile([P, 1], F32, name="first_factor")
         nc.scalar.activation(out=first_factor[:], in_=inv0[:], func=ACT.Copy, scale=sb_col[:, 0:1])
-        for h in range(2):
-            nc.scalar.activation(
-                out=pairs[h][:, 0, :, 0], in_=r_exp[0][:, h * HALF : (h + 1) * HALF], func=ACT.Copy, scale=first_factor[:]
-            )
-        scale_halves(nc.gpsimd, 2, invert_on_gpsimd(2)[:])
-        scale_halves(nc.gpsimd, 3, invert_on_gpsimd(3)[:])
+        scale_on_scalar(0, first_factor)
+        middle_inv = keep.tile([P, 2], F32, name="middle_inv")
+        nc.gpsimd.tensor_tensor(out=middle_inv[:], in0=b_sum[:, 2:4], in1=minus_one[:], op=ALU.pow)
+        for h in (1, 0):
+            for t in (2, 3):
+                scale_on_gpsimd(t, h, middle_inv[:, t - 2 : t - 1])
         last_negmax = keep.tile([P, 1], F32, name="last_negmax", tag="late_negmax")
         second_softmax(1, last_negmax[:])
 
@@ -216,7 +217,9 @@ def tile_attend_rollout_kernel(
 
         inv1 = keep.tile([P, 1], F32, name="inv1", tag="query_buffer", align_bytes=64)
         nc.vector.reciprocal(out=inv1[:], in_=b_sum[:, 1:2])
-        scale_halves(nc.vector, 1, inv1[:])
+        last_factor = keep.tile([P, 1], F32, name="last_factor")
+        nc.vector.tensor_tensor(out=last_factor[:], in0=inv1[:], in1=sb_col[:, 1:2], op=ALU.mult)
+        scale_on_scalar(1, last_factor)
         nc.vector.reciprocal(out=a_inv[:], in_=a_sum[:])
 
         wt_ps = psum.tile([P, 2, Q], F32, name="wt_ps", tag="bank_w")
@@ -231,7 +234,7 @@ def tile_attend_rollout_kernel(
 
         weigh_and_turn(0)
         weigh_and_turn(1)
-        wt_grp = keep.tile([P, Q, PACK], BF16, name="wt_grp", align_bytes=64)
+        wt_grp = keep.tile([P, Q, PACK], BF16, name="wt_grp", tag="wt_buffer", align_bytes=64)
         nc.scalar.copy(
             out=wt_grp[:].rearrange("p q t -> p (q t)").bitcast(F32).rearrange("p (q u) -> p q u", u=2),
             in_=wt_ps[:].rearrange("p u q -> p q u"),
@@ -239,23 +242,28 @@ def tile_attend_rollout_kernel(
         wt_codes = keep.tile([P, Q], U32, name="wt_codes", align_bytes=64)
         wt_sc = keep.tile([P, Q], U8, name="wt_sc", align_bytes=64)
 
-        x_grp, x_codes, x_sc = [], [], []
+        x_grp, x_sc = [], []
         for h in range(2):
             x_grp.append(keep.tile([P, HALF, PACK], BF16, name="x_grp%d" % h, align_bytes=64))
-            x_codes.append(keep.tile([P, HALF], U32, name="x_codes%d" % h, align_bytes=64))
             x_sc.append(keep.tile([P, HALF], U8, name="x_sc%d" % h, align_bytes=64))
-        for h in range(2):
-            nc.scalar.copy(
+        for h, copy in enumerate((nc.vector.tensor_copy, nc.scalar.copy)):
+            copy(
                 out=x_grp[h][:].rearrange("p j t -> p (j t)").bitcast(F32).rearrange("p (j u) -> p j u", u=2),
                 in_=pairs[h][:].rearrange("p u j e -> p (u j e)").bitcast(F32).rearrange("p (u j) -> p j u", u=2),
             )
-        for h in range(2):
+        x_codes = {}
+
+        def quantise_x(h, tag):
+            x_codes[h] = keep.tile([P, HALF], U32, name="x_codes%d" % h, tag=tag, align_bytes=64)
             nc.vector.quantize_mx(
                 out=x_codes[h][:].bitcast(FP8X4), scales=x_sc[h][:], in_=x_grp[h][:].rearrange("p j t -> p (j t)")
             )
-        nc.vector.quantize_mx(out=wt_codes[:].bitcast(FP8X4), scales=wt_sc[:], in_=wt_grp[:].rearrange("p q t -> p (q t)"))
 
-        for h, (bank, copy) in enumerate((("bank_a", nc.scalar.copy), ("bank_c", nc.vector.tensor_copy))):
+        quantise_x(1, "x_codes1")
+        nc.vector.quantize_mx(out=wt_codes[:].bitcast(FP8X4), scales=wt_sc[:], in_=wt_grp[:].rearrange("p q t -> p (q t)"))
+        quantise_x(0, "wt_buffer")
+
+        for h, bank, copy in ((1, "bank_a", nc.scalar.copy), (0, "bank_c", nc.vector.tensor_copy)):
             y_ps = psum.tile([P, HALF], F32, name="y_ps%d" % h, tag=bank)
             nc.tensor.matmul_mx(
                 out=y_ps[:], lhsT=wt_codes[:].bitcast(FP8X4), lhsT_scale=wt_sc[:],

@@ -85,7 +85,7 @@ def tile_attend_rollout_kernel(
         nc.gpsimd.memset(minus_one[:], -1.0)
 
         nc.sync.dma_start(offs_t[:], offs)
-        for queue, partition in ((nc.sync, 0), (nc.sync, SCALE_ROWS)):
+        for queue, partition in ((nc.scalar, 0), (nc.sync, SCALE_ROWS)):
             load_scale_rows(queue, qp_sc, qpool_scales, 0, SCALE_ROWS, partition)
         nc.sync.dma_start(offs2_t[:], offs2)
         for half in range(2):
@@ -218,7 +218,7 @@ def tile_attend_rollout_kernel(
         inv1 = keep.tile([P, 1], F32, name="inv1", tag="query_buffer", align_bytes=64)
         nc.vector.reciprocal(out=inv1[:], in_=b_sum[:, 1:2])
         last_factor = keep.tile([P, 1], F32, name="last_factor")
-        nc.vector.tensor_tensor(out=last_factor[:], in0=inv1[:], in1=sb_col[:, 1:2], op=ALU.mult)
+        nc.vector.tensor_scalar(out=last_factor[:], in0=inv1[:], scalar1=sb_col[:, 1:2], scalar2=None, op0=ALU.mult)
         scale_on_scalar(1, last_factor)
         nc.vector.reciprocal(out=a_inv[:], in_=a_sum[:])
 

@@ -17,7 +17,8 @@ AXIS_X = mybir.AxisListType.X
 P = 128
 QUAD = 32
 PACK = 4
-RUN = 4
+RUN = 8
+ROW = 4
 D, T, I, J, Q = 512, 2048, 512, 512, 128
 HALF = J // 2
 LIST_ROWS = 16
@@ -38,12 +39,19 @@ def load_scale_rows(queue, tile, scales, first_row, rows, partition):
     )
 
 
-def move_quadrant_rows(nc, plane, moves):
-    for quad, partition in moves:
-        nc.sync.dma_start(
-            out=plane[QUAD * quad : QUAD * quad + QUAD_ROWS, :].bitcast(I32),
-            in_=plane[partition : partition + QUAD_ROWS, :].bitcast(I32),
-        )
+def load_spread_rows(queue, tile, scales):
+    queue.dma_start(out=tile[0:P:ROW_STEP, :].bitcast(I32), in_=scales[0].bitcast(I32))
+
+
+def move_spread_rows(nc, plane, gathered):
+    for r in range(QUAD_ROWS):
+        nc.sync.dma_start(out=plane[r:P:QUAD, :].bitcast(I32), in_=gathered[ROW_STEP * r : P : QUAD, :].bitcast(I32))
+
+
+def spread_by_place(nc, bank, raw, ident):
+    dealt = bank[:].rearrange("q t (g h c) -> q c g t h", h=RUN // ROW, c=ROW)
+    for c in range(ROW):
+        nc.tensor.transpose(dealt[:, c], raw[:, c : c + 1].to_broadcast([P, P]), ident[:])
 
 
 def gather_halves(nc, pool, window, offsets, name):
@@ -69,70 +77,64 @@ def tile_attend_rollout_kernel(
         offs2_t = keep.tile([P, J // LIST_ROWS], U16, name="offs2_t")
         k_sc = keep.tile([P, T], U8, name="k_sc", align_bytes=64)
         qp_sc = keep.tile([P, T], U8, name="qp_sc", align_bytes=64)
-        k2_sc = keep.tile([P, T], U8, name="k2_sc", tag="keys2_scale_window", align_bytes=64)
+        k2_sc = big.tile([P, T], U8, name="k2_sc", tag="keys_window", align_bytes=64)
         ident = keep.tile([P, P], F32, name="ident")
-        sb_raw = keep.tile([P, RUN], F32, name="sb_raw")
+        sb_raw = keep.tile([P, ROW], F32, name="sb_raw")
         q_raw = keep.tile([P, PACK, Q], F32, name="q_raw")
         qp_w = big.tile([P, T], U32, name="qp_w")
         k2_w = big.tile([P, T], U32, name="k2_w", align_bytes=64)
 
-        nc.gpsimd.memset(k2_sc[:].bitcast(I32), 0)
+        nc.gpsimd.memset(qp_sc[:].bitcast(I32), 0)
+        nc.vector.memset(k2_sc[2 * QUAD : P, :].bitcast(I32), 0)
+        nc.vector.memset(k2_sc[QUAD : 2 * QUAD, :].bitcast(I32), 0)
         nc.vector.memset(k_sc[:].bitcast(I32), 0)
-        nc.vector.memset(qp_sc[2 * QUAD : P, :].bitcast(I32), 0)
-        nc.vector.memset(qp_sc[QUAD : 2 * QUAD, :].bitcast(I32), 0)
         make_identity(nc, ident[:])
         minus_one = keep.tile([P, 2], F32, name="minus_one")
         nc.gpsimd.memset(minus_one[:], -1.0)
 
-        nc.sync.dma_start(offs_t[:], offs)
-        for queue, partition in ((nc.scalar, 0), (nc.sync, SCALE_ROWS)):
-            load_scale_rows(queue, qp_sc, qpool_scales, 0, SCALE_ROWS, partition)
         nc.sync.dma_start(offs2_t[:], offs2)
-        for half in range(2):
-            load_scale_rows(nc.sync, k2_sc, keys2_scales, half * SCALE_ROWS // 2, SCALE_ROWS // 2, half * 2 * QUAD)
-        nc.sync.dma_start(out=k_sc[0:P:ROW_STEP, :].bitcast(I32), in_=keys_scales[0].bitcast(I32))
+        nc.sync.dma_start(
+            out=k2_sc[0:QUAD, :].bitcast(I32),
+            in_=keys2_scales[0].bitcast(I32).unsqueeze(1).broadcast_to([SCALE_ROWS, 2, T // 4]),
+        )
+        nc.sync.dma_start(offs_t[:], offs)
+        for quad in range(P // QUAD):
+            load_scale_rows((nc.scalar, nc.sync)[quad % 2], qp_sc, qpool_scales, QUAD_ROWS * quad, QUAD_ROWS, QUAD * quad)
         load_words(nc, qp_w, qpool_words)
-        nc.sync.dma_start(out=sb_raw[:], in_=sb.rearrange("(p r) o -> p (r o)", r=RUN))
+        load_spread_rows(nc.sync, k_sc, keys_scales)
+        nc.sync.dma_start(out=sb_raw[:], in_=sb.rearrange("(p r) o -> p (r o)", r=ROW))
         load_words(nc, k2_w, keys2_words)
         nc.sync.dma_start(out=q_raw[:], in_=query.rearrange("(p j) w -> p j w", j=PACK))
 
-        sb_ps = psum.tile([P, RUN, P], F32, name="sb_ps", tag="bank_w")
-        for r in range(RUN):
-            nc.tensor.transpose(sb_ps[:, r, :], sb_raw[:, r : r + 1].to_broadcast([P, P]), ident[:])
+        sb_ps = psum.tile([P, PACK, P], F32, name="sb_ps", tag="bank_w")
+        spread_by_place(nc, sb_ps, sb_raw, ident)
         sb_rows = keep.tile([P, PACK, P], F32, name="sb_rows")
-        nc.scalar.activation(
-            out=sb_rows[:].rearrange("q t (m r) -> q t m r", r=RUN),
-            in_=sb_ps[:].rearrange("q r (m t) -> q t m r", t=PACK), func=ACT.Copy, scale=OUT_FACTOR,
-        )
+        nc.scalar.activation(out=sb_rows[:], in_=sb_ps[:], func=ACT.Copy, scale=OUT_FACTOR)
         cols_ps = psum.tile([P, PACK, P], F32, name="cols_ps", tag="bank_c")
         for t in range(PACK):
             nc.tensor.transpose(cols_ps[:, t, :], sb_rows[:, t, :], ident[:])
         sb_col = keep.tile([P, PACK], F32, name="sb_col")
         nc.scalar.copy(out=sb_col[:], in_=cols_ps[:, :, 0])
 
-        qg_plain = keep.tile([P, I], U8, name="qg_plain", align_bytes=64)
-        nc.vector.tensor_copy(qg_plain[:], qp_sc[:].indirect(offs_t[:]))
-        k2g_plain = big.tile([P, J], U8, name="k2g_plain", tag="keys_window", align_bytes=64)
+        k2g_plain = keep.tile([P, J], U8, name="k2g_plain", align_bytes=64)
         nc.vector.tensor_copy(k2g_plain[:], k2_sc[:].indirect(offs2_t[:]))
-        qg_sc = keep.tile([P, I], U8, name="qg_sc", tag="keys2_scale_window", align_bytes=64)
-        nc.vector.tensor_copy(
-            out=qg_sc[:].bitcast(I32).rearrange("p (t m) -> p t m", t=PACK),
-            in_=qg_plain[:].bitcast(I32).rearrange("p (m t) -> p t m", t=PACK),
-        )
-        move_quadrant_rows(nc, qg_sc, [(quad, QUAD_ROWS * quad) for quad in (1, 2, 3)])
         k2g_sc = keep.tile([P, J], U8, name="k2g_sc", align_bytes=64)
-        nc.vector.tensor_copy(out=k2g_sc[:].bitcast(I32), in_=k2g_plain[:].bitcast(I32))
-        move_quadrant_rows(nc, k2g_sc, [(quad, QUAD * (quad - 1) + QUAD_ROWS) for quad in (1, 3)])
+        for quad in range(P // QUAD):
+            nc.sync.dma_start(
+                out=k2g_sc[QUAD * quad : QUAD * quad + QUAD_ROWS, :].bitcast(I32),
+                in_=k2g_plain[2 * QUAD_ROWS * quad : 2 * QUAD_ROWS * (quad + 1) : 2, :].bitcast(I32),
+            )
         k_w = big.tile([P, T], U32, name="k_w", tag="keys_window", align_bytes=64)
         load_words(nc, k_w, keys_words)
+        qg_sc = keep.tile([P, I], U8, name="qg_sc", align_bytes=64)
+        nc.vector.tensor_copy(qg_sc[:].rearrange("p (t g r) -> p g t r", t=PACK, r=RUN), qp_sc[:].indirect(offs_t[:]))
+
+        qg_w = keep.tile([P, I], U32, name="qg_w", align_bytes=64)
+        nc.vector.tensor_copy(qg_w[:].rearrange("p (t g r) -> p g t r", t=PACK, r=RUN), qp_w[:].indirect(offs_t[:]))
         kg_plain = keep.tile([P, I], U8, name="kg_plain", align_bytes=64)
         nc.vector.tensor_copy(kg_plain[:], k_sc[:].indirect(offs_t[:]))
         kg_sc = keep.tile([P, I], U8, name="kg_sc", align_bytes=64)
-        for r in range(QUAD_ROWS):
-            nc.sync.dma_start(out=kg_sc[r:P:QUAD, :].bitcast(I32), in_=kg_plain[ROW_STEP * r : P : QUAD, :].bitcast(I32))
-
-        qg_w = keep.tile([P, I], U32, name="qg_w", align_bytes=64)
-        nc.vector.tensor_copy(qg_w[:].rearrange("p (t m r) -> p m t r", t=PACK, r=RUN), qp_w[:].indirect(offs_t[:]))
+        move_spread_rows(nc, kg_sc, kg_plain)
         k2g_w = gather_halves(nc, keep, k2_w, offs2_t, "k2g_w")
         b_ps = [psum.tile([P, J], F32, name="b_ps%d" % t) for t in range(PACK)]
         for t in (0, 2, 3, 1):
@@ -149,8 +151,8 @@ def tile_attend_rollout_kernel(
         q_codes = keep.tile([P, Q], U32, name="q_codes", align_bytes=64)
         q_sc = keep.tile([P, Q], U8, name="q_sc", align_bytes=64)
         nc.vector.quantize_mx(out=q_codes[:].bitcast(FP8X4), scales=q_sc[:], in_=q_grp[:].rearrange("p w j -> p (w j)"))
-        sa_raw = keep.tile([P, RUN], F32, name="sa_raw", tag="query_buffer", align_bytes=64)
-        nc.sync.dma_start(out=sa_raw[:], in_=sa.rearrange("o (p r) -> p (o r)", r=RUN))
+        sa_raw = keep.tile([P, ROW], F32, name="sa_raw", tag="query_buffer", align_bytes=64)
+        nc.sync.dma_start(out=sa_raw[:], in_=sa.rearrange("o (p r) -> p (o r)", r=ROW))
         kg_w = gather_halves(nc, keep, k_w, offs_t, "kg_w")
 
         r_exp = [keep.tile([P, J], F32, name="r_exp%d" % t) for t in range(PACK)]
@@ -199,19 +201,16 @@ def tile_attend_rollout_kernel(
                 out=a_ps[:, h * HALF : (h + 1) * HALF], lhsT=q_codes[:].bitcast(FP8X4), lhsT_scale=q_sc[:],
                 rhs=kg_w[h][:].bitcast(FP8X4), rhs_scale=kg_sc[:, h * HALF : (h + 1) * HALF], start=True, stop=True,
             )
-        sa_ps = psum.tile([P, 2, P, 2], F32, name="sa_ps")
-        for r in range(RUN):
-            nc.tensor.transpose(
-                sa_ps[:].rearrange("q u (m r) e -> q r m u e", r=RUN)[:, r], sa_raw[:, r : r + 1].to_broadcast([P, P]), ident[:]
-            )
+        sa_ps = psum.tile([P, PACK, P], F32, name="sa_ps")
+        spread_by_place(nc, sa_ps, sa_raw, ident)
         a_negmax = keep.tile([P, 1], F32, name="a_negmax")
         a_sum = keep.tile([P, 1], F32, name="a_sum")
         a_inv = keep.tile([P, 1], F32, name="a_inv")
         nc.vector.tensor_reduce(out=a_negmax[:], in_=a_ps[:], axis=AXIS_X, op=ALU.max, negate=True)
         p_exp = keep.tile([P, PACK, P], F32, name="p_exp")
         nc.scalar.activation(
-            out=p_exp[:].rearrange("q t (m r) -> q t m r", r=RUN),
-            in_=a_ps[:].rearrange("q (m t r) -> q t m r", t=PACK, r=RUN),
+            out=p_exp[:].rearrange("q t (g r) -> q t g r", r=RUN),
+            in_=a_ps[:].rearrange("q (g t r) -> q t g r", t=PACK, r=RUN),
             func=ACT.Exp, bias=a_negmax[:], scale=1.0, accum_out=a_sum[:],
         )
 
@@ -228,7 +227,7 @@ def tile_attend_rollout_kernel(
             w_pair = keep.tile([P, P, 2], BF16, name="w_pair%d" % u, align_bytes=64)
             nc.vector.scalar_tensor_tensor(
                 out=w_pair[:], in0=p_exp[:, 2 * u : 2 * u + 2, :].rearrange("q e p -> q p e"), scalar=a_inv[:],
-                in1=sa_ps[:, u, :, :], op0=ALU.mult, op1=ALU.mult,
+                in1=sa_ps[:, 2 * u : 2 * u + 2, :].rearrange("q e p -> q p e"), op0=ALU.mult, op1=ALU.mult,
             )
             nc.tensor.transpose(wt_ps[:, u, :], w_pair[:].rearrange("q p e -> q (p e)").bitcast(F32), ident[:])
 

@@ -54,6 +54,14 @@ def spread_by_place(nc, bank, raw, ident):
         nc.tensor.transpose(dealt[:, c], raw[:, c : c + 1].to_broadcast([P, P]), ident[:])
 
 
+def move_quadrant_rows(nc, plane, moves):
+    for quad, partition in moves:
+        nc.sync.dma_start(
+            out=plane[QUAD * quad : QUAD * quad + QUAD_ROWS, :].bitcast(I32),
+            in_=plane[partition : partition + QUAD_ROWS, :].bitcast(I32),
+        )
+
+
 def gather_halves(nc, pool, window, offsets, name):
     columns = HALF // LIST_ROWS
     halves = []
@@ -77,32 +85,30 @@ def tile_attend_rollout_kernel(
         offs2_t = keep.tile([P, J // LIST_ROWS], U16, name="offs2_t")
         k_sc = keep.tile([P, T], U8, name="k_sc", align_bytes=64)
         qp_sc = keep.tile([P, T], U8, name="qp_sc", align_bytes=64)
-        k2_sc = big.tile([P, T], U8, name="k2_sc", tag="keys_window", align_bytes=64)
+        k2_sc = keep.tile([P, T], U8, name="k2_sc", tag="keys2_scale_window", align_bytes=64)
         ident = keep.tile([P, P], F32, name="ident")
         sb_raw = keep.tile([P, ROW], F32, name="sb_raw")
-        q_raw = keep.tile([P, PACK, Q], F32, name="q_raw")
+        q_raw = keep.tile([P, PACK, Q], F32, name="q_raw", tag="loaded_query", align_bytes=64)
         qp_w = big.tile([P, T], U32, name="qp_w")
         k2_w = big.tile([P, T], U32, name="k2_w", align_bytes=64)
 
-        nc.gpsimd.memset(qp_sc[:].bitcast(I32), 0)
-        nc.vector.memset(k2_sc[2 * QUAD : P, :].bitcast(I32), 0)
-        nc.vector.memset(k2_sc[QUAD : 2 * QUAD, :].bitcast(I32), 0)
+        nc.gpsimd.memset(k2_sc[:].bitcast(I32), 0)
         nc.vector.memset(k_sc[:].bitcast(I32), 0)
+        nc.vector.memset(qp_sc[2 * QUAD : P, :].bitcast(I32), 0)
+        nc.vector.memset(qp_sc[QUAD : 2 * QUAD, :].bitcast(I32), 0)
         make_identity(nc, ident[:])
         minus_one = keep.tile([P, 2], F32, name="minus_one")
         nc.gpsimd.memset(minus_one[:], -1.0)
 
-        nc.sync.dma_start(offs2_t[:], offs2)
-        nc.sync.dma_start(
-            out=k2_sc[0:QUAD, :].bitcast(I32),
-            in_=keys2_scales[0].bitcast(I32).unsqueeze(1).broadcast_to([SCALE_ROWS, 2, T // 4]),
-        )
         nc.sync.dma_start(offs_t[:], offs)
-        for quad in range(P // QUAD):
-            load_scale_rows((nc.scalar, nc.sync)[quad % 2], qp_sc, qpool_scales, QUAD_ROWS * quad, QUAD_ROWS, QUAD * quad)
+        for queue, partition in ((nc.scalar, 0), (nc.sync, SCALE_ROWS)):
+            load_scale_rows(queue, qp_sc, qpool_scales, 0, SCALE_ROWS, partition)
+        nc.sync.dma_start(offs2_t[:], offs2)
+        for half, queue in enumerate((nc.sync, nc.scalar)):
+            load_scale_rows(queue, k2_sc, keys2_scales, half * SCALE_ROWS // 2, SCALE_ROWS // 2, half * 2 * QUAD)
         load_words(nc, qp_w, qpool_words)
-        load_spread_rows(nc.sync, k_sc, keys_scales)
         nc.sync.dma_start(out=sb_raw[:], in_=sb.rearrange("(p r) o -> p (r o)", r=ROW))
+        load_spread_rows(nc.sync, k_sc, keys_scales)
         load_words(nc, k2_w, keys2_words)
         nc.sync.dma_start(out=q_raw[:], in_=query.rearrange("(p j) w -> p j w", j=PACK))
 
@@ -116,25 +122,35 @@ def tile_attend_rollout_kernel(
         sb_col = keep.tile([P, PACK], F32, name="sb_col")
         nc.scalar.copy(out=sb_col[:], in_=cols_ps[:, :, 0])
 
-        k2g_plain = keep.tile([P, J], U8, name="k2g_plain", align_bytes=64)
+        qg_plain = keep.tile([P, I], U8, name="qg_plain", align_bytes=64)
+        nc.vector.tensor_copy(qg_plain[:], qp_sc[:].indirect(offs_t[:]))
+        k2g_plain = big.tile([P, J], U8, name="k2g_plain", tag="keys_window", align_bytes=64)
         nc.vector.tensor_copy(k2g_plain[:], k2_sc[:].indirect(offs2_t[:]))
+        qg_sc = keep.tile([P, I], U8, name="qg_sc", tag="keys2_scale_window", align_bytes=64)
+        nc.vector.tensor_copy(
+            out=qg_sc[:].bitcast(I32).rearrange("p (t g c) -> p t g c", t=PACK, c=RUN // 4),
+            in_=qg_plain[:].bitcast(I32).rearrange("p (g t c) -> p t g c", t=PACK, c=RUN // 4),
+        )
+        move_quadrant_rows(nc, qg_sc, [(quad, QUAD_ROWS * quad) for quad in (1, 2, 3)])
         k2g_sc = keep.tile([P, J], U8, name="k2g_sc", align_bytes=64)
-        for quad in range(P // QUAD):
-            nc.sync.dma_start(
-                out=k2g_sc[QUAD * quad : QUAD * quad + QUAD_ROWS, :].bitcast(I32),
-                in_=k2g_plain[2 * QUAD_ROWS * quad : 2 * QUAD_ROWS * (quad + 1) : 2, :].bitcast(I32),
-            )
+        nc.vector.tensor_copy(out=k2g_sc[:].bitcast(I32), in_=k2g_plain[:].bitcast(I32))
+        move_quadrant_rows(nc, k2g_sc, [(quad, QUAD * (quad - 1) + QUAD_ROWS) for quad in (1, 3)])
         k_w = big.tile([P, T], U32, name="k_w", tag="keys_window", align_bytes=64)
         load_words(nc, k_w, keys_words)
-        qg_sc = keep.tile([P, I], U8, name="qg_sc", align_bytes=64)
-        nc.vector.tensor_copy(qg_sc[:].rearrange("p (t g r) -> p g t r", t=PACK, r=RUN), qp_sc[:].indirect(offs_t[:]))
 
         qg_w = keep.tile([P, I], U32, name="qg_w", align_bytes=64)
         nc.vector.tensor_copy(qg_w[:].rearrange("p (t g r) -> p g t r", t=PACK, r=RUN), qp_w[:].indirect(offs_t[:]))
-        kg_plain = keep.tile([P, I], U8, name="kg_plain", align_bytes=64)
-        nc.vector.tensor_copy(kg_plain[:], k_sc[:].indirect(offs_t[:]))
-        kg_sc = keep.tile([P, I], U8, name="kg_sc", align_bytes=64)
-        move_spread_rows(nc, kg_sc, kg_plain)
+        kg_sc = []
+
+        def gather_key_scales(h, tag):
+            columns = HALF // LIST_ROWS
+            plain = keep.tile([P, HALF], U8, name="kg_plain%d" % h, tag=tag, align_bytes=64)
+            nc.vector.tensor_copy(plain[:], k_sc[:].indirect(offs_t[:, h * columns : (h + 1) * columns]))
+            plane = keep.tile([P, HALF], U8, name="kg_sc%d" % h, align_bytes=64)
+            move_spread_rows(nc, plane, plain)
+            kg_sc.append(plane)
+
+        gather_key_scales(0, "kg_plain0")
         k2g_w = gather_halves(nc, keep, k2_w, offs2_t, "k2g_w")
         b_ps = [psum.tile([P, J], F32, name="b_ps%d" % t) for t in range(PACK)]
         for t in (0, 2, 3, 1):
@@ -148,6 +164,7 @@ def tile_attend_rollout_kernel(
 
         q_grp = keep.tile([P, Q, PACK], BF16, name="q_grp", tag="query_buffer", align_bytes=64)
         nc.scalar.copy(out=q_grp[:], in_=q_raw[:].rearrange("p j w -> p w j"))
+        gather_key_scales(1, "loaded_query")
         q_codes = keep.tile([P, Q], U32, name="q_codes", align_bytes=64)
         q_sc = keep.tile([P, Q], U8, name="q_sc", align_bytes=64)
         nc.vector.quantize_mx(out=q_codes[:].bitcast(FP8X4), scales=q_sc[:], in_=q_grp[:].rearrange("p w j -> p (w j)"))
@@ -199,7 +216,7 @@ def tile_attend_rollout_kernel(
         for h in range(2):
             nc.tensor.matmul_mx(
                 out=a_ps[:, h * HALF : (h + 1) * HALF], lhsT=q_codes[:].bitcast(FP8X4), lhsT_scale=q_sc[:],
-                rhs=kg_w[h][:].bitcast(FP8X4), rhs_scale=kg_sc[:, h * HALF : (h + 1) * HALF], start=True, stop=True,
+                rhs=kg_w[h][:].bitcast(FP8X4), rhs_scale=kg_sc[h][:], start=True, stop=True,
             )
         sa_ps = psum.tile([P, PACK, P], F32, name="sa_ps")
         spread_by_place(nc, sa_ps, sa_raw, ident)

@@ -88,7 +88,7 @@ def tile_attend_rollout_kernel(
         k2_sc = keep.tile([P, T], U8, name="k2_sc", tag="keys2_scale_window", align_bytes=64)
         ident = keep.tile([P, P], F32, name="ident")
         sb_raw = keep.tile([P, ROW], F32, name="sb_raw")
-        q_raw = keep.tile([P, PACK, Q], F32, name="q_raw", tag="loaded_query", align_bytes=64)
+        q_raw = keep.tile([P, PACK, Q], F32, name="q_raw")
         qp_w = big.tile([P, T], U32, name="qp_w")
         k2_w = big.tile([P, T], U32, name="k2_w", align_bytes=64)
 
@@ -107,8 +107,8 @@ def tile_attend_rollout_kernel(
         for half, queue in enumerate((nc.sync, nc.scalar)):
             load_scale_rows(queue, k2_sc, keys2_scales, half * SCALE_ROWS // 2, SCALE_ROWS // 2, half * 2 * QUAD)
         load_words(nc, qp_w, qpool_words)
-        nc.sync.dma_start(out=sb_raw[:], in_=sb.rearrange("(p r) o -> p (r o)", r=ROW))
         load_spread_rows(nc.sync, k_sc, keys_scales)
+        nc.sync.dma_start(out=sb_raw[:], in_=sb.rearrange("(p r) o -> p (r o)", r=ROW))
         load_words(nc, k2_w, keys2_words)
         nc.sync.dma_start(out=q_raw[:], in_=query.rearrange("(p j) w -> p j w", j=PACK))
 
@@ -140,17 +140,10 @@ def tile_attend_rollout_kernel(
 
         qg_w = keep.tile([P, I], U32, name="qg_w", align_bytes=64)
         nc.vector.tensor_copy(qg_w[:].rearrange("p (t g r) -> p g t r", t=PACK, r=RUN), qp_w[:].indirect(offs_t[:]))
-        kg_sc = []
-
-        def gather_key_scales(h, tag):
-            columns = HALF // LIST_ROWS
-            plain = keep.tile([P, HALF], U8, name="kg_plain%d" % h, tag=tag, align_bytes=64)
-            nc.vector.tensor_copy(plain[:], k_sc[:].indirect(offs_t[:, h * columns : (h + 1) * columns]))
-            plane = keep.tile([P, HALF], U8, name="kg_sc%d" % h, align_bytes=64)
-            move_spread_rows(nc, plane, plain)
-            kg_sc.append(plane)
-
-        gather_key_scales(0, "kg_plain0")
+        kg_plain = keep.tile([P, I], U8, name="kg_plain", align_bytes=64)
+        nc.vector.tensor_copy(kg_plain[:], k_sc[:].indirect(offs_t[:]))
+        kg_sc = keep.tile([P, I], U8, name="kg_sc", align_bytes=64)
+        move_spread_rows(nc, kg_sc, kg_plain)
         k2g_w = gather_halves(nc, keep, k2_w, offs2_t, "k2g_w")
         b_ps = [psum.tile([P, J], F32, name="b_ps%d" % t) for t in range(PACK)]
         for t in (0, 2, 3, 1):
@@ -164,7 +157,6 @@ def tile_attend_rollout_kernel(
 
         q_grp = keep.tile([P, Q, PACK], BF16, name="q_grp", tag="query_buffer", align_bytes=64)
         nc.scalar.copy(out=q_grp[:], in_=q_raw[:].rearrange("p j w -> p w j"))
-        gather_key_scales(1, "loaded_query")
         q_codes = keep.tile([P, Q], U32, name="q_codes", align_bytes=64)
         q_sc = keep.tile([P, Q], U8, name="q_sc", align_bytes=64)
         nc.vector.quantize_mx(out=q_codes[:].bitcast(FP8X4), scales=q_sc[:], in_=q_grp[:].rearrange("p w j -> p (w j)"))
@@ -216,7 +208,7 @@ def tile_attend_rollout_kernel(
         for h in range(2):
             nc.tensor.matmul_mx(
                 out=a_ps[:, h * HALF : (h + 1) * HALF], lhsT=q_codes[:].bitcast(FP8X4), lhsT_scale=q_sc[:],
-                rhs=kg_w[h][:].bitcast(FP8X4), rhs_scale=kg_sc[h][:], start=True, stop=True,
+                rhs=kg_w[h][:].bitcast(FP8X4), rhs_scale=kg_sc[:, h * HALF : (h + 1) * HALF], start=True, stop=True,
             )
         sa_ps = psum.tile([P, PACK, P], F32, name="sa_ps")
         spread_by_place(nc, sa_ps, sa_raw, ident)

@@ -101,7 +101,7 @@ def tile_attend_rollout_kernel(
         nc.gpsimd.memset(minus_one[:], -1.0)
 
         nc.sync.dma_start(offs_t[:], offs)
-        for queue, partition in ((nc.scalar, 0), (nc.sync, SCALE_ROWS)):
+        for queue, partition in ((nc.scalar, 0), (nc.scalar, SCALE_ROWS)):
             load_scale_rows(queue, qp_sc, qpool_scales, 0, SCALE_ROWS, partition)
         nc.sync.dma_start(offs2_t[:], offs2)
         for half, queue in enumerate((nc.sync, nc.scalar)):

from contextlib import ExitStack

import concourse.mybir as mybir
from concourse.masks import make_identity

F32 = mybir.dt.float32
BF16 = mybir.dt.bfloat16
I32 = mybir.dt.int32
U32 = mybir.dt.uint32
U16 = mybir.dt.uint16
U8 = mybir.dt.uint8
FP8X4 = mybir.dt.float8_e4m3fn_x4
ALU = mybir.AluOpType
ACT = mybir.ActivationFunctionType
AXIS_X = mybir.AxisListType.X

P = 128
QUAD = 32
PACK = 4
RUN = 8
ROW = 4
D, T, I, J, Q = 512, 2048, 512, 512, 128
HALF = J // 2
LIST_ROWS = 16
SCALE_ROWS = 16
QUAD_ROWS = 4
ROW_STEP = P // SCALE_ROWS
OUT_FACTOR = 512.0
FLOPS = 2 * D * Q * I + 2 * D * I * J + 2 * I * Q * J


def load_words(nc, tile, words):
    nc.sync.dma_start(out=tile[:].bitcast(I32), in_=words[0].rearrange("p n t -> p (n t)").bitcast(I32))


def load_scale_rows(queue, tile, scales, first_row, rows, partition):
    queue.dma_start(
        out=tile[partition : partition + rows, :].bitcast(I32), in_=scales[0].bitcast(I32)[first_row : first_row + rows, :]
    )


def load_spread_rows(queue, tile, scales):
    queue.dma_start(out=tile[0:P:ROW_STEP, :].bitcast(I32), in_=scales[0].bitcast(I32))


def move_spread_rows(nc, plane, gathered):
    for r in range(QUAD_ROWS):
        nc.sync.dma_start(out=plane[r:P:QUAD, :].bitcast(I32), in_=gathered[ROW_STEP * r : P : QUAD, :].bitcast(I32))


def spread_by_place(nc, bank, raw, ident):
    dealt = bank[:].rearrange("q t (g h c) -> q c g t h", h=RUN // ROW, c=ROW)
    for c in range(ROW):
        nc.tensor.transpose(dealt[:, c], raw[:, c : c + 1].to_broadcast([P, P]), ident[:])


def move_quadrant_rows(nc, plane, moves):
    for quad, partition in moves:
        nc.sync.dma_start(
            out=plane[QUAD * quad : QUAD * quad + QUAD_ROWS, :].bitcast(I32),
            in_=plane[partition : partition + QUAD_ROWS, :].bitcast(I32),
        )


def gather_halves(nc, pool, window, offsets, name):
    columns = HALF // LIST_ROWS
    halves = []
    for h in range(2):
        part = pool.tile([P, HALF], U32, name="%s%d" % (name, h), align_bytes=64)
        nc.vector.tensor_copy(part[:], window[:].indirect(offsets[:, h * columns : (h + 1) * columns]))
        halves.append(part)
    return halves


def tile_attend_rollout_kernel(
    tc, query, keys_words, keys_scales, qpool_words, qpool_scales, keys2_words, keys2_scales, sa, sb, offs, offs2, out
):
    nc = tc.nc
    with ExitStack() as ctx:
        keep = ctx.enter_context(tc.tile_pool(name="keep", bufs=1))
        big = ctx.enter_context(tc.tile_pool(name="big", bufs=1))
        psum = ctx.enter_context(tc.psum_pool(name="psum", bufs=1))

        offs_t = keep.tile([P, I // LIST_ROWS], U16, name="offs_t")
        offs2_t = keep.tile([P, J // LIST_ROWS], U16, name="offs2_t")
        k_sc = keep.tile([P, T], U8, name="k_sc", align_bytes=64)
        qp_sc = keep.tile([P, T], U8, name="qp_sc", align_bytes=64)
        k2_sc = keep.tile([P, T], U8, name="k2_sc", tag="keys2_scale_window", align_bytes=64)
        ident = keep.tile([P, P], F32, name="ident")
        sb_raw = keep.tile([P, ROW], F32, name="sb_raw")
        q_raw = keep.tile([P, PACK, Q], F32, name="q_raw")
        qp_w = big.tile([P, T], U32, name="qp_w")
        k2_w = big.tile([P, T], U32, name="k2_w", align_bytes=64)

        nc.gpsimd.memset(k2_sc[:].bitcast(I32), 0)
        nc.vector.memset(k_sc[:].bitcast(I32), 0)
        nc.vector.memset(qp_sc[2 * QUAD : P, :].bitcast(I32), 0)
        nc.vector.memset(qp_sc[QUAD : 2 * QUAD, :].bitcast(I32), 0)
        make_identity(nc, ident[:])
        minus_one = keep.tile([P, 2], F32, name="minus_one")
        nc.gpsimd.memset(minus_one[:], -1.0)

        nc.sync.dma_start(offs_t[:], offs)
        for queue, partition in ((nc.scalar, 0), (nc.scalar, SCALE_ROWS)):
            load_scale_rows(queue, qp_sc, qpool_scales, 0, SCALE_ROWS, partition)
        nc.sync.dma_start(offs2_t[:], offs2)
        for half, queue in enumerate((nc.sync, nc.scalar)):
            load_scale_rows(queue, k2_sc, keys2_scales, half * SCALE_ROWS // 2, SCALE_ROWS // 2, half * 2 * QUAD)
        load_words(nc, qp_w, qpool_words)
        load_spread_rows(nc.sync, k_sc, keys_scales)
        nc.sync.dma_start(out=sb_raw[:], in_=sb.rearrange("(p r) o -> p (r o)", r=ROW))
        load_words(nc, k2_w, keys2_words)
        nc.sync.dma_start(out=q_raw[:], in_=query.rearrange("(p j) w -> p j w", j=PACK))

        sb_ps = psum.tile([P, PACK, P], F32, name="sb_ps", tag="bank_w")
        spread_by_place(nc, sb_ps, sb_raw, ident)
        sb_rows = keep.tile([P, PACK, P], F32, name="sb_rows")
        nc.scalar.activation(out=sb_rows[:], in_=sb_ps[:], func=ACT.Copy, scale=OUT_FACTOR)
        cols_ps = psum.tile([P, PACK, P], F32, name="cols_ps", tag="bank_c")
        for t in range(PACK):
            nc.tensor.transpose(cols_ps[:, t, :], sb_rows[:, t, :], ident[:])
        sb_col = keep.tile([P, PACK], F32, name="sb_col")
        nc.scalar.copy(out=sb_col[:], in_=cols_ps[:, :, 0])

        qg_plain = keep.tile([P, I], U8, name="qg_plain", align_bytes=64)
        nc.vector.tensor_copy(qg_plain[:], qp_sc[:].indirect(offs_t[:]))
        k2g_plain = big.tile([P, J], U8, name="k2g_plain", tag="keys_window", align_bytes=64)
        nc.vector.tensor_copy(k2g_plain[:], k2_sc[:].indirect(offs2_t[:]))
        qg_sc = keep.tile([P, I], U8, name="qg_sc", tag="keys2_scale_window", align_bytes=64)
        nc.vector.tensor_copy(
            out=qg_sc[:].bitcast(I32).rearrange("p (t g c) -> p t g c", t=PACK, c=RUN // 4),
            in_=qg_plain[:].bitcast(I32).rearrange("p (g t c) -> p t g c", t=PACK, c=RUN // 4),
        )
        move_quadrant_rows(nc, qg_sc, [(quad, QUAD_ROWS * quad) for quad in (1, 2, 3)])
        k2g_sc = keep.tile([P, J], U8, name="k2g_sc", align_bytes=64)
        nc.vector.tensor_copy(out=k2g_sc[:].bitcast(I32), in_=k2g_plain[:].bitcast(I32))
        move_quadrant_rows(nc, k2g_sc, [(quad, QUAD * (quad - 1) + QUAD_ROWS) for quad in (1, 3)])
        k_w = big.tile([P, T], U32, name="k_w", tag="keys_window", align_bytes=64)
        load_words(nc, k_w, keys_words)

        qg_w = keep.tile([P, I], U32, name="qg_w", align_bytes=64)
        nc.vector.tensor_copy(qg_w[:].rearrange("p (t g r) -> p g t r", t=PACK, r=RUN), qp_w[:].indirect(offs_t[:]))
        kg_plain = keep.tile([P, I], U8, name="kg_plain", align_bytes=64)
        nc.vector.tensor_copy(kg_plain[:], k_sc[:].indirect(offs_t[:]))
        kg_sc = keep.tile([P, I], U8, name="kg_sc", align_bytes=64)
        move_spread_rows(nc, kg_sc, kg_plain)
        k2g_w = gather_halves(nc, keep, k2_w, offs2_t, "k2g_w")
        b_ps = [psum.tile([P, J], F32, name="b_ps%d" % t) for t in range(PACK)]
        for t in (0, 2, 3, 1):
            for h in range(2):
                nc.tensor.matmul_mx(
                    out=b_ps[t][:, h * HALF : (h + 1) * HALF],
                    lhsT=qg_w[:, t * P : (t + 1) * P].bitcast(FP8X4), lhsT_scale=qg_sc[:, t * P : (t + 1) * P],
                    rhs=k2g_w[h][:].bitcast(FP8X4), rhs_scale=k2g_sc[:, h * HALF : (h + 1) * HALF],
                    start=True, stop=True,
                )

        q_grp = keep.tile([P, Q, PACK], BF16, name="q_grp", tag="query_buffer", align_bytes=64)
        nc.scalar.copy(out=q_grp[:], in_=q_raw[:].rearrange("p j w -> p w j"))
        q_codes = keep.tile([P, Q], U32, name="q_codes", align_bytes=64)
        q_sc = keep.tile([P, Q], U8, name="q_sc", align_bytes=64)
        nc.vector.quantize_mx(out=q_codes[:].bitcast(FP8X4), scales=q_sc[:], in_=q_grp[:].rearrange("p w j -> p (w j)"))
        sa_raw = keep.tile([P, ROW], F32, name="sa_raw", tag="query_buffer", align_bytes=64)
        nc.sync.dma_start(out=sa_raw[:], in_=sa.rearrange("o (p r) -> p (o r)", r=ROW))
        kg_w = gather_halves(nc, keep, k_w, offs_t, "kg_w")

        r_exp = [keep.tile([P, J], F32, name="r_exp%d" % t) for t in range(PACK)]
        b_sum = keep.tile([P, PACK], F32, name="b_sum")
        pairs = [keep.tile([P, 2, HALF, 2], BF16, name="pairs%d" % h, align_bytes=64) for h in range(2)]

        def second_softmax(t, negmax):
            nc.vector.tensor_reduce(out=negmax, in_=b_ps[t][:], axis=AXIS_X, op=ALU.max, negate=True)
            nc.scalar.activation(
                out=r_exp[t][:], in_=b_ps[t][:], func=ACT.Exp, bias=negmax, scale=1.0, accum_out=b_sum[:, t : t + 1]
            )

        def scale_on_gpsimd(t, h, inv):
            nc.gpsimd.tensor_scalar(
                out=pairs[h][:, t // 2, :, t % 2], in0=r_exp[t][:, h * HALF : (h + 1) * HALF],
                scalar1=inv, scalar2=sb_col[:, t : t + 1], op0=ALU.mult, op1=ALU.mult,
            )

        def scale_on_scalar(t, factor):
            for h in (1, 0):
                nc.scalar.activation(
                    out=pairs[h][:, t // 2, :, t % 2], in_=r_exp[t][:, h * HALF : (h + 1) * HALF], func=ACT.Copy, scale=factor[:]
                )

        early_negmax = keep.tile([P, 2], F32, name="early_negmax")
        second_softmax(0, early_negmax[:, 0:1])
        second_softmax(2, early_negmax[:, 1:2])
        third_negmax = keep.tile([P, 1], F32, name="third_negmax", tag="late_negmax")
        second_softmax(3, third_negmax[:])
        inv0 = keep.tile([P, 1], F32, name="inv0")
        nc.gpsimd.tensor_tensor(out=inv0[:], in0=b_sum[:, 0:1], in1=minus_one[:, 0:1], op=ALU.pow)
        first_factor = keep.tile([P, 1], F32, name="first_factor")
        nc.scalar.activation(out=first_factor[:], in_=inv0[:], func=ACT.Copy, scale=sb_col[:, 0:1])
        scale_on_scalar(0, first_factor)
        middle_inv = keep.tile([P, 2], F32, name="middle_inv")
        nc.gpsimd.tensor_tensor(out=middle_inv[:], in0=b_sum[:, 2:4], in1=minus_one[:], op=ALU.pow)
        for h in (1, 0):
            for t in (2, 3):
                scale_on_gpsimd(t, h, middle_inv[:, t - 2 : t - 1])
        last_negmax = keep.tile([P, 1], F32, name="last_negmax", tag="late_negmax")
        second_softmax(1, last_negmax[:])

        a_ps = psum.tile([P, I], F32, name="a_ps", tag="bank_a")
        for h in range(2):
            nc.tensor.matmul_mx(
                out=a_ps[:, h * HALF : (h + 1) * HALF], lhsT=q_codes[:].bitcast(FP8X4), lhsT_scale=q_sc[:],
                rhs=kg_w[h][:].bitcast(FP8X4), rhs_scale=kg_sc[:, h * HALF : (h + 1) * HALF], start=True, stop=True,
            )
        sa_ps = psum.tile([P, PACK, P], F32, name="sa_ps")
        spread_by_place(nc, sa_ps, sa_raw, ident)
        a_negmax = keep.tile([P, 1], F32, name="a_negmax")
        a_sum = keep.tile([P, 1], F32, name="a_sum")
        a_inv = keep.tile([P, 1], F32, name="a_inv")
        nc.vector.tensor_reduce(out=a_negmax[:], in_=a_ps[:], axis=AXIS_X, op=ALU.max, negate=True)
        p_exp = keep.tile([P, PACK, P], F32, name="p_exp")
        nc.scalar.activation(
            out=p_exp[:].rearrange("q t (g r) -> q t g r", r=RUN),
            in_=a_ps[:].rearrange("q (g t r) -> q t g r", t=PACK, r=RUN),
            func=ACT.Exp, bias=a_negmax[:], scale=1.0, accum_out=a_sum[:],
        )

        inv1 = keep.tile([P, 1], F32, name="inv1", tag="query_buffer", align_bytes=64)
        nc.vector.reciprocal(out=inv1[:], in_=b_sum[:, 1:2])
        last_factor = keep.tile([P, 1], F32, name="last_factor")
        nc.vector.tensor_scalar(out=last_factor[:], in0=inv1[:], scalar1=sb_col[:, 1:2], scalar2=None, op0=ALU.mult)
        scale_on_scalar(1, last_factor)
        nc.vector.reciprocal(out=a_inv[:], in_=a_sum[:])

        wt_ps = psum.tile([P, 2, Q], F32, name="wt_ps", tag="bank_w")

        def weigh_and_turn(u):
            w_pair = keep.tile([P, P, 2], BF16, name="w_pair%d" % u, align_bytes=64)
            nc.vector.scalar_tensor_tensor(
                out=w_pair[:], in0=p_exp[:, 2 * u : 2 * u + 2, :].rearrange("q e p -> q p e"), scalar=a_inv[:],
                in1=sa_ps[:, 2 * u : 2 * u + 2, :].rearrange("q e p -> q p e"), op0=ALU.mult, op1=ALU.mult,
            )
            nc.tensor.transpose(wt_ps[:, u, :], w_pair[:].rearrange("q p e -> q (p e)").bitcast(F32), ident[:])

        weigh_and_turn(0)
        weigh_and_turn(1)
        wt_grp = keep.tile([P, Q, PACK], BF16, name="wt_grp", tag="wt_buffer", align_bytes=64)
        nc.scalar.copy(
            out=wt_grp[:].rearrange("p q t -> p (q t)").bitcast(F32).rearrange("p (q u) -> p q u", u=2),
            in_=wt_ps[:].rearrange("p u q -> p q u"),
        )
        wt_codes = keep.tile([P, Q], U32, name="wt_codes", align_bytes=64)
        wt_sc = keep.tile([P, Q], U8, name="wt_sc", align_bytes=64)

        x_grp, x_sc = [], []
        for h in range(2):
            x_grp.append(keep.tile([P, HALF, PACK], BF16, name="x_grp%d" % h, align_bytes=64))
            x_sc.append(keep.tile([P, HALF], U8, name="x_sc%d" % h, align_bytes=64))
        for h, copy in enumerate((nc.vector.tensor_copy, nc.scalar.copy)):
            copy(
                out=x_grp[h][:].rearrange("p j t -> p (j t)").bitcast(F32).rearrange("p (j u) -> p j u", u=2),
                in_=pairs[h][:].rearrange("p u j e -> p (u j e)").bitcast(F32).rearrange("p (u j) -> p j u", u=2),
            )
        x_codes = {}

        def quantise_x(h, tag):
            x_codes[h] = keep.tile([P, HALF], U32, name="x_codes%d" % h, tag=tag, align_bytes=64)
            nc.vector.quantize_mx(
                out=x_codes[h][:].bitcast(FP8X4), scales=x_sc[h][:], in_=x_grp[h][:].rearrange("p j t -> p (j t)")
            )

        quantise_x(1, "x_codes1")
        nc.vector.quantize_mx(out=wt_codes[:].bitcast(FP8X4), scales=wt_sc[:], in_=wt_grp[:].rearrange("p q t -> p (q t)"))
        quantise_x(0, "wt_buffer")

        for h, bank, copy in ((1, "bank_a", nc.scalar.copy), (0, "bank_c", nc.vector.tensor_copy)):
            y_ps = psum.tile([P, HALF], F32, name="y_ps%d" % h, tag=bank)
            nc.tensor.matmul_mx(
                out=y_ps[:], lhsT=wt_codes[:].bitcast(FP8X4), lhsT_scale=wt_sc[:],
                rhs=x_codes[h][:].bitcast(FP8X4), rhs_scale=x_sc[h][:], start=True, stop=True,
            )
            y_sb = keep.tile([P, HALF], F32, name="y_sb%d" % h)
            copy(out=y_sb[:], in_=y_ps[:])
            nc.sync.dma_start(out=out[:, h * HALF : (h + 1) * HALF], in_=y_sb[:])
